import numpy as np
import ml_dtypes


def mxq(x, axis, fmt="e4m3"):
    dtype, down = {"e4m3": (ml_dtypes.float8_e4m3fn, 7), "e5m2": (ml_dtypes.float8_e5m2, 14)}[fmt]
    v = np.moveaxis(np.asarray(x, np.float32).astype(ml_dtypes.bfloat16).astype(np.float64), axis, -1)
    blocks = v.reshape(v.shape[:-1] + (-1, 32))
    amax = np.abs(blocks).max(-1, keepdims=True)
    byte = np.maximum(np.where(amax > 0, np.frexp(amax)[1] - 1 + 127, 0) - down, 1)
    scale = np.exp2(byte - 127.0)
    codes = (blocks / scale).astype(np.float32).astype(dtype).astype(np.float64)
    return np.moveaxis((codes * scale).reshape(v.shape), -1, axis)


WIDE = False


def mx_kscale(k):
    if not WIDE:
        return np.ones(k)
    levels = np.array([10, -10, 5, -5, 0])
    if k % 512:
        return np.exp2(np.random.permutation(np.resize(levels, k // 32))).repeat(32)
    a = np.empty((k // 512, 16))
    for p in range(k // 512):
        a[p, :8] = np.random.permutation(np.resize(levels, 8))
        for g in range(8):
            far = levels[np.abs(levels - a[p, g]) >= 10]
            a[p, g + 8] = far[np.random.randint(len(far))]
    return np.exp2(a.ravel()).repeat(32)


def f64(x):
    return np.asarray(x).astype(np.float64)


def striped(idx):
    return np.tile(idx.reshape(-1, 16).T, (8, 1)).astype(np.uint16)


def unstriped(offs):
    return offs[:16].T.reshape(-1).astype(np.int64)


def pack_weight(w):
    k, n = w.shape
    w = f64(np.asarray(w, np.float32).astype(ml_dtypes.bfloat16)).reshape(k // 32, 32, n)
    amax = np.abs(w).max(1)
    byte = np.clip(np.where(amax > 0, np.frexp(amax)[1] - 1 + 127 - 7, 1), 1, 254)
    scaled = (w * np.exp2(127.0 - byte)[:, None, :]).reshape(k, n).astype(np.float32)
    words = np.ascontiguousarray(scaled.reshape(k // 512, 128, 4, n).transpose(0, 1, 3, 2)).astype(ml_dtypes.float8_e4m3fn).view(np.uint8)
    return words, np.ascontiguousarray(byte.astype(np.uint8).reshape(k // 512, 16, n))


def unpack_weight(words, scales):
    g, p, n, _ = words.shape
    vals = np.ascontiguousarray(words).view(ml_dtypes.float8_e4m3fn).astype(np.float64) * np.repeat(np.exp2(scales.astype(np.float64) - 127.0), 8, axis=1)[..., None]
    return vals.transpose(0, 1, 3, 2).reshape(g * 512, n)


def sigmoid(v):
    return 1.0 / (1.0 + np.exp(-np.maximum(v, -700.0)))


K, T, S, V = 1024, 2048, 512, 512


def setup_inputs():
    n = np.random.standard_normal
    s = mx_kscale(K)[:, None]
    packed_xT = pack_weight(n((K, T)) * s)
    return {
        "x_words": packed_xT[0],
        "x_scales": packed_xT[1],
        "w1": (n((K, K)) / K / s / s.T).astype(np.float32),
        "offs": striped(np.random.permutation(T)[:S]),
        "dst": striped(np.random.permutation(T)[:V]),
    }


def reference(x_words, x_scales, w1, offs, dst):
    xq = unpack_weight(x_words, x_scales)[:, unstriped(offs)]
    z = mxq(f64(w1), 0, "e4m3").T @ xq
    x_dst = unpack_weight(x_words, x_scales)[:, unstriped(dst)]
    y = mxq(z, 0, "e4m3").T @ x_dst
    return sigmoid(y)

@@ -1,0 +1,200 @@
+from contextlib import ExitStack
+
+import concourse.mybir as mybir
+
+F32 = mybir.dt.float32
+BF16 = mybir.dt.bfloat16
+I32 = mybir.dt.int32
+U32 = mybir.dt.uint32
+U16 = mybir.dt.uint16
+U8 = mybir.dt.uint8
+FP8X4 = mybir.dt.float8_e4m3fn_x4
+SIGMOID = mybir.ActivationFunctionType.Sigmoid
+
+P = 128
+PACK = 4
+PASS = P * PACK
+K, T, S, V = 1024, 2048, 512, 512
+PASSES = K // PASS
+TILES = S // P
+FLOPS = 2 * K * K * S + 2 * K * S * V
+
+CHUNKS = {
+    (0, 0): [(0, 64, 0), (64, 128, 64)],
+    (0, 1): [(0, 64, 0), (64, 128, 108)],
+    (1, 0): [(0, 64, 44), (64, 128, 108)],
+    (1, 1): [(0, 64, 44), (64, 128, 108)],
+}
+
+
+def tile_picked_zresc_sig_p_kernel(tc, x_words, x_scales, w1, offs, dst, out):
+    nc = tc.nc
+    with ExitStack() as ctx:
+        keep = ctx.enter_context(tc.tile_pool(name="keep", bufs=1))
+        psum = ctx.enter_context(tc.psum_pool(name="psum", bufs=1))
+
+        lists = [keep.tile([P, S // 16], U16, name="offs_sb"), keep.tile([P, V // 16], U16, name="dst_sb")]
+        table = [keep.tile([P, T], I32, name=f"table{g}", align_bytes=64) for g in range(PASSES)]
+        table_scale = keep.tile([P, T], U8, name="table_scale", align_bytes=64)
+        picked = [[keep.tile([P, S], U32, name=f"picked{u}{g}", align_bytes=64) for g in range(PASSES)] for u in range(2)]
+        picked_scale = [keep.tile([P, S], U8, name=f"picked_scale{u}", align_bytes=64) for u in range(2)]
+        w_raw, w_bf, w_q, w_s = {}, {}, {}, {}
+        for (b, g), chunks in CHUNKS.items():
+            for c, (m0, m1, ms) in enumerate(chunks):
+                w_raw[b, g, c] = keep.tile([P, PACK, PACK * (m1 - m0)], F32, name=f"w_raw{b}{g}{c}", align_bytes=64)
+            w_bf[b, g] = keep.tile([P, PACK, P, PACK], BF16, name=f"w_bf{b}{g}", align_bytes=64)
+            w_q[b, g] = keep.tile([P, PASS], U32, name=f"w_q{b}{g}", align_bytes=64)
+            w_s[b, g] = keep.tile([P, PASS], U8, name=f"w_s{b}{g}", align_bytes=64)
+        y_bank = [psum.tile([P, V], F32, name=f"y_bank{t}") for t in range(TILES)]
+
+        def load_table(g, pieces):
+            words = x_words[g].rearrange("p n r -> p (n r)").bitcast(I32)
+            width = T // pieces
+            for i in range(pieces):
+                cols = slice(width * i, width * (i + 1))
+                nc.sync.dma_start(out=table[g][:, cols], in_=words[:, cols])
+
+        def load_scales():
+            nc.vector.memset(table_scale[:].bitcast(I32), 0)
+            for q in range(4):
+                nc.sync.dma_start(
+                    out=table_scale[32 * q : 32 * q + 8, :].bitcast(I32),
+                    in_=x_scales[:, 4 * q : 4 * q + 4, :].bitcast(I32),
+                )
+
+        def load_w(b, g):
+            rows = w1[PASS * g : PASS * (g + 1), :].rearrange("(p j) c -> p j c", j=PACK)
+            for c, (m0, m1, ms) in enumerate(CHUNKS[b, g]):
+                nc.sync.dma_start(out=w_raw[b, g, c][:], in_=rows[:, :, PASS * b + PACK * m0 : PASS * b + PACK * m1])
+
+        def gather_words(u, g):
+            nc.vector.tensor_copy(picked[u][g][:], table[g][:].bitcast(U32).indirect(lists[u][:]))
+
+        def gather_scales(u):
+            nc.vector.tensor_copy(picked_scale[u][:], table_scale[:].indirect(lists[u][:]))
+
+        def cast_w(b, g, c):
+            m0, m1, ms = CHUNKS[b, g][c]
+            src = w_raw[b, g, c][:].rearrange("p j (m t) -> p m j t", t=PACK)
+            dealt = w_bf[b, g][:].rearrange("p t m j -> p m j t")
+            if ms > m0:
+                nc.vector.tensor_copy(out=dealt[:, m0:ms], in_=src[:, 0 : ms - m0])
+            if m1 > ms:
+                nc.scalar.copy(out=dealt[:, ms:m1], in_=src[:, ms - m0 : m1 - m0])
+
+        def quantize_w(b, g, pieces):
+            flat = w_bf[b, g][:].rearrange("p t m j -> p (t m j)")
+            width = PASS // pieces
+            for i in range(pieces):
+                cols = slice(width * i, width * (i + 1))
+                nc.vector.quantize_mx(
+                    out=w_q[b, g][:, cols].bitcast(FP8X4),
+                    scales=w_s[b, g][:, cols],
+                    in_=flat[:, PACK * width * i : PACK * width * (i + 1)],
+                )
+
+        z_bank, z_bf, z_q, z_s = {}, {}, {}, {}
+
+        def z_pass(b, t, j, g):
+            if (b, t) not in z_bank:
+                z_bank[b, t] = psum.tile([P, PACK, P], F32, name=f"z_bank{b}{t}", tag=f"z_bank{t}")
+            cols = slice(P * j, P * (j + 1))
+            toks = slice(P * t, P * (t + 1))
+            nc.tensor.matmul_mx(
+                out=z_bank[b, t][:, j, :],
+                lhsT=w_q[b, g][:, cols].bitcast(FP8X4),
+                lhsT_scale=w_s[b, g][:, cols],
+                rhs=picked[0][g][:, toks].bitcast(FP8X4),
+                rhs_scale=picked_scale[0][4 * g : P, toks],
+                start=(g == 0),
+                stop=(g == PASSES - 1),
+            )
+
+        def z_rest(b, t):
+            z_pass(b, t, 0, 1)
+            for j in range(1, PACK):
+                for g in range(PASSES):
+                    z_pass(b, t, j, g)
+
+        def z_round(b, t, engine_copy):
+            z_bf[b, t] = keep.tile([P, P, PACK], BF16, name=f"z_bf{b}{t}", align_bytes=64)
+            engine_copy(out=z_bf[b, t][:], in_=z_bank[b, t][:].rearrange("p j n -> p n j"))
+
+        def z_quantize(b, t):
+            z_q[b, t] = keep.tile([P, P], U32, name=f"z_q{b}{t}", align_bytes=64)
+            z_s[b, t] = keep.tile([P, P], U8, name=f"z_s{b}{t}", align_bytes=64)
+            nc.vector.quantize_mx(
+                out=z_q[b, t][:].bitcast(FP8X4),
+                scales=z_s[b, t][:],
+                in_=z_bf[b, t][:].rearrange("p n j -> p (n j)"),
+            )
+
+        def y_pass(b, t):
+            nc.tensor.matmul_mx(
+                out=y_bank[t][:],
+                lhsT=z_q[b, t][:].bitcast(FP8X4),
+                lhsT_scale=z_s[b, t][:],
+                rhs=picked[1][b][:].bitcast(FP8X4),
+                rhs_scale=picked_scale[1][4 * b : P, :],
+                start=(b == 0),
+                stop=(b == PASSES - 1),
+            )
+
+        def finish(t):
+            result = keep.tile([P, V], F32, name=f"result{t}")
+            nc.scalar.activation(out=result[:], in_=y_bank[t][:], func=SIGMOID)
+            nc.sync.dma_start(out=out[P * t : P * (t + 1), :], in_=result[:])
+
+        nc.sync.dma_start(lists[0][:], offs)
+        nc.sync.dma_start(lists[1][:], dst)
+        load_table(0, 4)
+        load_scales()
+        load_w(0, 0)
+        load_table(1, 1)
+        load_w(0, 1)
+        load_w(1, 0)
+        load_w(1, 1)
+
+        gather_words(0, 0)
+        gather_words(1, 0)
+        gather_scales(0)
+        gather_scales(1)
+        cast_w(0, 0, 0)
+        cast_w(0, 0, 1)
+        gather_words(0, 1)
+        quantize_w(0, 0, 1)
+        gather_words(1, 1)
+        for t in range(TILES):
+            z_pass(0, t, 0, 0)
+        for t in range(TILES):
+            nc.tensor.matmul_mx(
+                out=y_bank[t][:],
+                lhsT=w_q[0, 0][:, 0:P].bitcast(FP8X4),
+                lhsT_scale=w_s[0, 0][:, 0:P],
+                rhs=picked[0][1][:].bitcast(FP8X4),
+                rhs_scale=picked_scale[0][4:P, :],
+                start=True,
+                stop=True,
+            )
+        cast_w(0, 1, 0)
+        cast_w(0, 1, 1)
+        quantize_w(0, 1, 4)
+        cast_w(1, 0, 0)
+        for t in range(TILES):
+            z_rest(0, t)
+            z_round(0, t, nc.scalar.copy)
+            z_quantize(0, t)
+        cast_w(1, 0, 1)
+        quantize_w(1, 0, 1)
+        cast_w(1, 1, 0)
+        for t in range(TILES):
+            y_pass(0, t)
+            z_pass(1, t, 0, 0)
+        cast_w(1, 1, 1)
+        quantize_w(1, 1, 4)
+        for t in range(TILES):
+            z_rest(1, t)
+            z_round(1, t, nc.scalar.copy if t < 2 else nc.vector.tensor_copy)
+            z_quantize(1, t)
+            y_pass(1, t)
+            finish(t)

@@ -20,10 +20,10 @@ TILES = S // P
 FLOPS = 2 * K * K * S + 2 * K * S * V
 
 CHUNKS = {
-    (0, 0): [(0, 64, 0), (64, 128, 64)],
-    (0, 1): [(0, 64, 0), (64, 128, 108)],
-    (1, 0): [(0, 64, 44), (64, 128, 108)],
-    (1, 1): [(0, 64, 44), (64, 128, 108)],
+    (0, 0): [(0, 128, 0)],
+    (0, 1): [(0, 128, 64)],
+    (1, 0): [(0, 128, 80)],
+    (1, 1): [(0, 80, 80), (80, 128, 128)],
 }
 
 
@@ -41,11 +41,11 @@ def tile_picked_zresc_sig_p_kernel(tc, x_words, x_scales, w1, offs, dst, out):
         w_raw, w_bf, w_q, w_s = {}, {}, {}, {}
         for (b, g), chunks in CHUNKS.items():
             for c, (m0, m1, ms) in enumerate(chunks):
-                w_raw[b, g, c] = keep.tile([P, PACK, PACK * (m1 - m0)], F32, name=f"w_raw{b}{g}{c}", align_bytes=64)
-            w_bf[b, g] = keep.tile([P, PACK, P, PACK], BF16, name=f"w_bf{b}{g}", align_bytes=64)
+                w_raw[b, g, c] = keep.tile([P, PACK, PACK * (m1 - m0)], F32, name=f"w_raw{b}{g}{c}", tag=f"w_raw{b}{g}{c}", align_bytes=64)
+            w_bf[b, g] = keep.tile([P, PACK, P, PACK], BF16, name=f"w_bf{b}{g}", tag=f"w_bf{b}{g}", align_bytes=64)
             w_q[b, g] = keep.tile([P, PASS], U32, name=f"w_q{b}{g}", align_bytes=64)
             w_s[b, g] = keep.tile([P, PASS], U8, name=f"w_s{b}{g}", align_bytes=64)
-        y_bank = [psum.tile([P, V], F32, name=f"y_bank{t}") for t in range(TILES)]
+        y_bank = {}
 
         def load_table(g, pieces):
             words = x_words[g].rearrange("p n r -> p (n r)").bitcast(I32)
@@ -54,12 +54,11 @@ def tile_picked_zresc_sig_p_kernel(tc, x_words, x_scales, w1, offs, dst, out):
                 cols = slice(width * i, width * (i + 1))
                 nc.sync.dma_start(out=table[g][:, cols], in_=words[:, cols])
 
-        def load_scales():
-            nc.vector.memset(table_scale[:].bitcast(I32), 0)
-            for q in range(4):
+        def load_scales(g):
+            for r in range(4):
                 nc.sync.dma_start(
-                    out=table_scale[32 * q : 32 * q + 8, :].bitcast(I32),
-                    in_=x_scales[:, 4 * q : 4 * q + 4, :].bitcast(I32),
+                    out=table_scale[4 * g + r : P : 32, :].bitcast(I32),
+                    in_=x_scales[g, r:16:4, :].bitcast(I32),
                 )
 
         def load_w(b, g):
@@ -97,7 +96,7 @@ def tile_picked_zresc_sig_p_kernel(tc, x_words, x_scales, w1, offs, dst, out):
 
         def z_pass(b, t, j, g):
             if (b, t) not in z_bank:
-                z_bank[b, t] = psum.tile([P, PACK, P], F32, name=f"z_bank{b}{t}", tag=f"z_bank{t}")
+                z_bank[b, t] = psum.tile([P, PACK, P], F32, name=f"z_bank{b}{t}", tag=f"bank{b}{t}")
             cols = slice(P * j, P * (j + 1))
             toks = slice(P * t, P * (t + 1))
             nc.tensor.matmul_mx(
@@ -106,95 +105,127 @@ def tile_picked_zresc_sig_p_kernel(tc, x_words, x_scales, w1, offs, dst, out):
                 lhsT_scale=w_s[b, g][:, cols],
                 rhs=picked[0][g][:, toks].bitcast(FP8X4),
                 rhs_scale=picked_scale[0][4 * g : P, toks],
-                start=(g == 0),
-                stop=(g == PASSES - 1),
+                start=(g == 0 and j == 0),
+                stop=(g == PASSES - 1 and j == PACK - 1),
             )
-
-        def z_rest(b, t):
-            z_pass(b, t, 0, 1)
-            for j in range(1, PACK):
-                for g in range(PASSES):
-                    z_pass(b, t, j, g)
 
         def z_round(b, t, engine_copy):
-            z_bf[b, t] = keep.tile([P, P, PACK], BF16, name=f"z_bf{b}{t}", align_bytes=64)
-            engine_copy(out=z_bf[b, t][:], in_=z_bank[b, t][:].rearrange("p j n -> p n j"))
+            first, count = z_group(b, t)
+            if t == first:
+                tag = "w_raw100" if b == 0 else f"z_bf{b}{t}"
+                z_bf[b, first] = keep.tile([P, count * P, PACK], BF16, name=f"z_bf{b}{t}", tag=tag, align_bytes=64)
+            toks = slice(P * (t - first), P * (t - first + 1))
+            engine_copy(out=z_bf[b, first][:, toks, :], in_=z_bank[b, t][:].rearrange("p j n -> p n j"))
 
-        def z_quantize(b, t):
-            z_q[b, t] = keep.tile([P, P], U32, name=f"z_q{b}{t}", align_bytes=64)
-            z_s[b, t] = keep.tile([P, P], U8, name=f"z_s{b}{t}", align_bytes=64)
+        def z_group(b, t):
+            return (0, TILES) if b == 0 else (t, 1)
+
+        def z_quantize(b, first):
+            count = z_group(b, first)[1]
+            tag = "w_bf11" if b == 0 else f"z_q{b}{first}"
+            codes = keep.tile([P, count * P], U32, name=f"z_q{b}{first}", tag=tag, align_bytes=64)
+            scales = keep.tile([P, count * P], U8, name=f"z_s{b}{first}", align_bytes=64)
             nc.vector.quantize_mx(
-                out=z_q[b, t][:].bitcast(FP8X4),
-                scales=z_s[b, t][:],
-                in_=z_bf[b, t][:].rearrange("p n j -> p (n j)"),
+                out=codes[:].bitcast(FP8X4),
+                scales=scales[:],
+                in_=z_bf[b, first][:].rearrange("p n j -> p (n j)"),
             )
+            for i in range(count):
+                z_q[b, first + i] = codes[:, P * i : P * (i + 1)]
+                z_s[b, first + i] = scales[:, P * i : P * (i + 1)]
 
         def y_pass(b, t):
+            if t not in y_bank:
+                y_bank[t] = psum.tile([P, V], F32, name=f"y_bank{t}", tag=f"bank0{t}")
             nc.tensor.matmul_mx(
                 out=y_bank[t][:],
-                lhsT=z_q[b, t][:].bitcast(FP8X4),
-                lhsT_scale=z_s[b, t][:],
+                lhsT=z_q[b, t].bitcast(FP8X4),
+                lhsT_scale=z_s[b, t],
                 rhs=picked[1][b][:].bitcast(FP8X4),
                 rhs_scale=picked_scale[1][4 * b : P, :],
                 start=(b == 0),
                 stop=(b == PASSES - 1),
             )
 
-        def finish(t):
-            result = keep.tile([P, V], F32, name=f"result{t}")
-            nc.scalar.activation(out=result[:], in_=y_bank[t][:], func=SIGMOID)
-            nc.sync.dma_start(out=out[P * t : P * (t + 1), :], in_=result[:])
+        def finish(t, pieces):
+            width = V // pieces
+            for i in range(pieces):
+                cols = slice(width * i, width * (i + 1))
+                result = keep.tile([P, width], F32, name=f"result{t}{i}")
+                nc.scalar.activation(out=result[:], in_=y_bank[t][:, cols], func=SIGMOID)
+                nc.sync.dma_start(out=out[P * t : P * (t + 1), cols], in_=result[:])
 
+        warm = keep.tile([P, 16], F32, name="warm")
+        nc.gpsimd.memset(warm[:, 0:8], 0.0)
+        nc.scalar.activation(out=warm[:, 8:16], in_=warm[:, 0:8], func=SIGMOID)
+        nc.vector.memset(table_scale[:].bitcast(I32), 0)
+        load_table(0, 1)
         nc.sync.dma_start(lists[0][:], offs)
         nc.sync.dma_start(lists[1][:], dst)
-        load_table(0, 4)
-        load_scales()
-        load_w(0, 0)
+        load_scales(0)
         load_table(1, 1)
+        load_scales(1)
+        load_w(0, 0)
         load_w(0, 1)
         load_w(1, 0)
         load_w(1, 1)
 
         gather_words(0, 0)
         gather_words(1, 0)
+        gather_words(0, 1)
+        gather_words(1, 1)
         gather_scales(0)
         gather_scales(1)
-        cast_w(0, 0, 0)
-        cast_w(0, 0, 1)
-        gather_words(0, 1)
-        quantize_w(0, 0, 1)
-        gather_words(1, 1)
-        for t in range(TILES):
-            z_pass(0, t, 0, 0)
-        for t in range(TILES):
+        z_bank[1, 0] = psum.tile([P, PACK, P], F32, name="z_bank10", tag="bank10")
+        for i in range(3):
             nc.tensor.matmul_mx(
-                out=y_bank[t][:],
-                lhsT=w_q[0, 0][:, 0:P].bitcast(FP8X4),
-                lhsT_scale=w_s[0, 0][:, 0:P],
+                out=z_bank[1, 0][:].rearrange("p j n -> p (j n)"),
+                lhsT=picked[0][0][:, 0:P].bitcast(FP8X4),
+                lhsT_scale=picked_scale[0][:, 0:P],
                 rhs=picked[0][1][:].bitcast(FP8X4),
                 rhs_scale=picked_scale[0][4:P, :],
                 start=True,
                 stop=True,
             )
+        cast_w(0, 0, 0)
+        quantize_w(0, 0, 1)
+        for t in range(TILES):
+            for j in range(PACK):
+                z_pass(0, t, j, 0)
         cast_w(0, 1, 0)
-        cast_w(0, 1, 1)
-        quantize_w(0, 1, 4)
+        quantize_w(0, 1, 2)
+        for t in range(TILES):
+            for j in range(PACK):
+                z_pass(0, t, j, 1)
         cast_w(1, 0, 0)
         for t in range(TILES):
-            z_rest(0, t)
             z_round(0, t, nc.scalar.copy)
-            z_quantize(0, t)
-        cast_w(1, 0, 1)
         quantize_w(1, 0, 1)
+        for t in range(TILES):
+            for j in range(PACK):
+                z_pass(1, t, j, 0)
         cast_w(1, 1, 0)
-        for t in range(TILES):
-            y_pass(0, t)
-            z_pass(1, t, 0, 0)
         cast_w(1, 1, 1)
-        quantize_w(1, 1, 4)
-        for t in range(TILES):
-            z_rest(1, t)
-            z_round(1, t, nc.scalar.copy if t < 2 else nc.vector.tensor_copy)
+        quantize_w(1, 1, 2)
+        for half in (0, 2):
+            for t in (0, 1):
+                z_pass(1, t, half, 1)
+                z_pass(1, t, half + 1, 1)
+        for t in (2, 3):
+            for j in range(PACK):
+                z_pass(1, t, j, 1)
+        z_quantize(0, 0)
+        z_round(1, 0, nc.scalar.copy)
+        z_round(1, 1, nc.vector.tensor_copy)
+        z_round(1, 2, nc.scalar.copy)
+        for t in (0, 1):
             z_quantize(1, t)
+            y_pass(0, t)
             y_pass(1, t)
-            finish(t)
+        z_round(1, 3, nc.vector.tensor_copy)
+        for t in (2, 3):
+            z_quantize(1, t)
+            y_pass(0, t)
+            y_pass(1, t)
+        for t in range(TILES):
+            finish(t, 2 if t == TILES - 1 else 1)

@@ -76,10 +76,11 @@ def tile_picked_zresc_sig_p_kernel(tc, x_words, x_scales, w1, offs, dst, out):
             m0, m1, ms = CHUNKS[b, g][c]
             src = w_raw[b, g, c][:].rearrange("p j (m t) -> p m j t", t=PACK)
             dealt = w_bf[b, g][:].rearrange("p t m j -> p m j t")
-            if ms > m0:
-                nc.vector.tensor_copy(out=dealt[:, m0:ms], in_=src[:, 0 : ms - m0])
-            if m1 > ms:
-                nc.scalar.copy(out=dealt[:, ms:m1], in_=src[:, ms - m0 : m1 - m0])
+            for pair in (slice(0, 2), slice(2, 4)):
+                if ms > m0:
+                    nc.vector.tensor_copy(out=dealt[:, m0:ms, :, pair], in_=src[:, 0 : ms - m0, :, pair])
+                if m1 > ms:
+                    nc.scalar.copy(out=dealt[:, ms:m1, :, pair], in_=src[:, ms - m0 : m1 - m0, :, pair])
 
         def quantize_w(b, g, pieces):
             flat = w_bf[b, g][:].rearrange("p t m j -> p (t m j)")

@@ -54,12 +54,13 @@ def tile_picked_zresc_sig_p_kernel(tc, x_words, x_scales, w1, offs, dst, out):
                 cols = slice(width * i, width * (i + 1))
                 nc.sync.dma_start(out=table[g][:, cols], in_=words[:, cols])
 
-        def load_scales(g):
-            for r in range(4):
-                nc.sync.dma_start(
-                    out=table_scale[4 * g + r : P : 32, :].bitcast(I32),
-                    in_=x_scales[g, r:16:4, :].bitcast(I32),
-                )
+        def load_scales(half):
+            for r in (2 * half, 2 * half + 1):
+                for g in range(PASSES):
+                    nc.sync.dma_start(
+                        out=table_scale[4 * g + r : P : 32, :].bitcast(I32),
+                        in_=x_scales[g, r:16:4, :].bitcast(I32),
+                    )
 
         def load_w(b, g):
             rows = w1[PASS * g : PASS * (g + 1), :].rearrange("(p j) c -> p j c", j=PACK)

@@ -73,15 +73,18 @@ def tile_picked_zresc_sig_p_kernel(tc, x_words, x_scales, w1, offs, dst, out):
         def gather_scales(u):
             nc.vector.tensor_copy(picked_scale[u][:], table_scale[:].indirect(lists[u][:]))
 
-        def cast_w(b, g, c):
+        def cast_w(b, g, c, parts=1):
             m0, m1, ms = CHUNKS[b, g][c]
-            src = w_raw[b, g, c][:].rearrange("p j (m t) -> p m j t", t=PACK)
-            dealt = w_bf[b, g][:].rearrange("p t m j -> p m j t")
-            for pair in (slice(0, 2), slice(2, 4)):
-                if ms > m0:
-                    nc.vector.tensor_copy(out=dealt[:, m0:ms, :, pair], in_=src[:, 0 : ms - m0, :, pair])
-                if m1 > ms:
-                    nc.scalar.copy(out=dealt[:, ms:m1, :, pair], in_=src[:, ms - m0 : m1 - m0, :, pair])
+            src = w_raw[b, g, c][:].rearrange("p j (m e t) -> p m j e t", e=2, t=PACK)
+            dealt = w_bf[b, g][:].rearrange("p t (m e) j -> p m j e t", e=2)
+            h0, h1, hs = m0 // 2, m1 // 2, ms // 2
+            width = PACK // parts
+            for i in range(parts):
+                outs = slice(width * i, width * (i + 1))
+                if hs > h0:
+                    nc.vector.tensor_copy(out=dealt[:, h0:hs, :, :, outs], in_=src[:, 0 : hs - h0, :, :, outs])
+                if h1 > hs:
+                    nc.scalar.copy(out=dealt[:, hs:h1, :, :, outs], in_=src[:, hs - h0 : h1 - h0, :, :, outs])
 
         def quantize_w(b, g, pieces):
             flat = w_bf[b, g][:].rearrange("p t m j -> p (t m j)")
@@ -194,7 +197,7 @@ def tile_picked_zresc_sig_p_kernel(tc, x_words, x_scales, w1, offs, dst, out):
         for t in range(TILES):
             for j in range(PACK):
                 z_pass(0, t, j, 0)
-        cast_w(0, 1, 0)
+        cast_w(0, 1, 0, 2)
         quantize_w(0, 1, 2)
         for t in range(TILES):
             for j in range(PACK):
@@ -207,7 +210,7 @@ def tile_picked_zresc_sig_p_kernel(tc, x_words, x_scales, w1, offs, dst, out):
             for j in range(PACK):
                 z_pass(1, t, j, 0)
         cast_w(1, 1, 0)
-        cast_w(1, 1, 1)
+        cast_w(1, 1, 1, 2)
         quantize_w(1, 1, 2)
         for half in (0, 2):
             for t in (0, 1):

@@ -20,10 +20,10 @@ TILES = S // P
 FLOPS = 2 * K * K * S + 2 * K * S * V
 
 CHUNKS = {
-    (0, 0): [(0, 128, 0)],
-    (0, 1): [(0, 128, 64)],
-    (1, 0): [(0, 128, 80)],
-    (1, 1): [(0, 80, 80), (80, 128, 128)],
+    (0, 0): [(0, 128, 56)],
+    (0, 1): [(0, 80, 40), (80, 128, 112)],
+    (1, 0): [(0, 80, 80), (80, 128, 128)],
+    (1, 1): [(0, 80, 64), (80, 128, 116)],
 }
 
 
@@ -35,13 +35,12 @@ def tile_picked_zresc_sig_p_kernel(tc, x_words, x_scales, w1, offs, dst, out):
 
         lists = [keep.tile([P, S // 16], U16, name="offs_sb"), keep.tile([P, V // 16], U16, name="dst_sb")]
         table = [keep.tile([P, T], I32, name=f"table{g}", align_bytes=64) for g in range(PASSES)]
-        table_scale = keep.tile([P, T], U8, name="table_scale", align_bytes=64)
+        table_scale = keep.tile([P, T], U8, name="table_scale", tag="w_raw010", align_bytes=64)
         picked = [[keep.tile([P, S], U32, name=f"picked{u}{g}", align_bytes=64) for g in range(PASSES)] for u in range(2)]
-        picked_scale = [keep.tile([P, S], U8, name=f"picked_scale{u}", align_bytes=64) for u in range(2)]
+        staged_scale = keep.tile([P, 2 * S], U8, name="staged_scale", align_bytes=64)
+        planes = keep.tile([P, 2 * S], U8, name="planes", align_bytes=64)
         w_raw, w_bf, w_q, w_s = {}, {}, {}, {}
         for (b, g), chunks in CHUNKS.items():
-            for c, (m0, m1, ms) in enumerate(chunks):
-                w_raw[b, g, c] = keep.tile([P, PACK, PACK * (m1 - m0)], F32, name=f"w_raw{b}{g}{c}", tag=f"w_raw{b}{g}{c}", align_bytes=64)
             w_bf[b, g] = keep.tile([P, PACK, P, PACK], BF16, name=f"w_bf{b}{g}", tag=f"w_bf{b}{g}", align_bytes=64)
             w_q[b, g] = keep.tile([P, PASS], U32, name=f"w_q{b}{g}", align_bytes=64)
             w_s[b, g] = keep.tile([P, PASS], U8, name=f"w_s{b}{g}", align_bytes=64)
@@ -54,24 +53,31 @@ def tile_picked_zresc_sig_p_kernel(tc, x_words, x_scales, w1, offs, dst, out):
                 cols = slice(width * i, width * (i + 1))
                 nc.sync.dma_start(out=table[g][:, cols], in_=words[:, cols])
 
-        def load_scales(half):
-            for r in (2 * half, 2 * half + 1):
-                for g in range(PASSES):
-                    nc.sync.dma_start(
-                        out=table_scale[4 * g + r : P : 32, :].bitcast(I32),
-                        in_=x_scales[g, r:16:4, :].bitcast(I32),
-                    )
+        def load_scales():
+            for g in range(PASSES):
+                nc.sync.dma_start(
+                    out=table_scale[16 * g : 16 * (g + 1), :].bitcast(I32),
+                    in_=x_scales[g].bitcast(I32).rearrange("(q r) n -> r q n", r=4),
+                )
+
+        def place_scales():
+            for q in range(4):
+                nc.scalar.dma_start(
+                    out=planes[32 * q : 32 * q + 8, :].bitcast(I32),
+                    in_=staged_scale[q:32:4, :].bitcast(I32),
+                )
 
         def load_w(b, g):
             rows = w1[PASS * g : PASS * (g + 1), :].rearrange("(p j) c -> p j c", j=PACK)
             for c, (m0, m1, ms) in enumerate(CHUNKS[b, g]):
+                w_raw[b, g, c] = keep.tile([P, PACK, PACK * (m1 - m0)], F32, name=f"w_raw{b}{g}{c}", tag=f"w_raw{b}{g}{c}", align_bytes=64)
                 nc.sync.dma_start(out=w_raw[b, g, c][:], in_=rows[:, :, PASS * b + PACK * m0 : PASS * b + PACK * m1])
 
         def gather_words(u, g):
             nc.vector.tensor_copy(picked[u][g][:], table[g][:].bitcast(U32).indirect(lists[u][:]))
 
         def gather_scales(u):
-            nc.vector.tensor_copy(picked_scale[u][:], table_scale[:].indirect(lists[u][:]))
+            nc.vector.tensor_copy(staged_scale[:, S * u : S * (u + 1)], table_scale[:].indirect(lists[u][:]))
 
         def cast_w(b, g, c, parts=1):
             m0, m1, ms = CHUNKS[b, g][c]
@@ -109,7 +115,7 @@ def tile_picked_zresc_sig_p_kernel(tc, x_words, x_scales, w1, offs, dst, out):
                 lhsT=w_q[b, g][:, cols].bitcast(FP8X4),
                 lhsT_scale=w_s[b, g][:, cols],
                 rhs=picked[0][g][:, toks].bitcast(FP8X4),
-                rhs_scale=picked_scale[0][4 * g : P, toks],
+                rhs_scale=planes[4 * g : P, toks],
                 start=(g == 0 and j == 0),
                 stop=(g == PASSES - 1 and j == PACK - 1),
             )
@@ -117,17 +123,17 @@ def tile_picked_zresc_sig_p_kernel(tc, x_words, x_scales, w1, offs, dst, out):
         def z_round(b, t, engine_copy):
             first, count = z_group(b, t)
             if t == first:
-                tag = "w_raw100" if b == 0 else f"z_bf{b}{t}"
+                tag = f"z_bf{b}{t}"
                 z_bf[b, first] = keep.tile([P, count * P, PACK], BF16, name=f"z_bf{b}{t}", tag=tag, align_bytes=64)
             toks = slice(P * (t - first), P * (t - first + 1))
             engine_copy(out=z_bf[b, first][:, toks, :], in_=z_bank[b, t][:].rearrange("p j n -> p n j"))
 
         def z_group(b, t):
-            return (0, TILES) if b == 0 else (t, 1)
+            return (t - t % 2, 2) if b == 0 else (t, 1)
 
         def z_quantize(b, first):
             count = z_group(b, first)[1]
-            tag = "w_bf11" if b == 0 else f"z_q{b}{first}"
+            tag = f"w_bf1{first // 2}" if b == 0 else f"z_q{b}{first}"
             codes = keep.tile([P, count * P], U32, name=f"z_q{b}{first}", tag=tag, align_bytes=64)
             scales = keep.tile([P, count * P], U8, name=f"z_s{b}{first}", align_bytes=64)
             nc.vector.quantize_mx(
@@ -147,7 +153,7 @@ def tile_picked_zresc_sig_p_kernel(tc, x_words, x_scales, w1, offs, dst, out):
                 lhsT=z_q[b, t].bitcast(FP8X4),
                 lhsT_scale=z_s[b, t],
                 rhs=picked[1][b][:].bitcast(FP8X4),
-                rhs_scale=picked_scale[1][4 * b : P, :],
+                rhs_scale=planes[4 * b : P, S : 2 * S],
                 start=(b == 0),
                 stop=(b == PASSES - 1),
             )
@@ -163,14 +169,18 @@ def tile_picked_zresc_sig_p_kernel(tc, x_words, x_scales, w1, offs, dst, out):
         warm = keep.tile([P, 16], F32, name="warm")
         nc.gpsimd.memset(warm[:, 0:8], 0.0)
         nc.scalar.activation(out=warm[:, 8:16], in_=warm[:, 0:8], func=SIGMOID)
-        nc.vector.memset(table_scale[:].bitcast(I32), 0)
-        load_table(0, 1)
+        nc.vector.memset(table_scale[32:64, :].bitcast(I32), 0)
+        nc.vector.memset(table_scale[64:P, :].bitcast(I32), 0)
+        nc.vector.memset(planes[:].bitcast(I32), 0)
+        load_scales()
         nc.sync.dma_start(lists[0][:], offs)
         nc.sync.dma_start(lists[1][:], dst)
-        load_scales(0)
+        load_table(0, 1)
         load_table(1, 1)
-        load_scales(1)
         load_w(0, 0)
+        gather_scales(0)
+        gather_scales(1)
+        place_scales()
         load_w(0, 1)
         load_w(1, 0)
         load_w(1, 1)
@@ -179,47 +189,50 @@ def tile_picked_zresc_sig_p_kernel(tc, x_words, x_scales, w1, offs, dst, out):
         gather_words(1, 0)
         gather_words(0, 1)
         gather_words(1, 1)
-        gather_scales(0)
-        gather_scales(1)
         z_bank[1, 0] = psum.tile([P, PACK, P], F32, name="z_bank10", tag="bank10")
-        for i in range(3):
+        for i in range(6):
             nc.tensor.matmul_mx(
                 out=z_bank[1, 0][:].rearrange("p j n -> p (j n)"),
                 lhsT=picked[0][0][:, 0:P].bitcast(FP8X4),
-                lhsT_scale=picked_scale[0][:, 0:P],
-                rhs=picked[0][1][:].bitcast(FP8X4),
-                rhs_scale=picked_scale[0][4:P, :],
+                lhsT_scale=staged_scale[:, 0:P],
+                rhs=picked[1][0][:].bitcast(FP8X4),
+                rhs_scale=staged_scale[:, S : 2 * S],
                 start=True,
                 stop=True,
             )
+
+        def closing(b):
+            for half in (0, 2):
+                for t in (0, 1):
+                    z_pass(b, t, half, 1)
+                    z_pass(b, t, half + 1, 1)
+            for t in (2, 3):
+                for j in range(PACK):
+                    z_pass(b, t, j, 1)
+
         cast_w(0, 0, 0)
         quantize_w(0, 0, 1)
         for t in range(TILES):
             for j in range(PACK):
                 z_pass(0, t, j, 0)
-        cast_w(0, 1, 0, 2)
+        cast_w(0, 1, 0)
+        cast_w(0, 1, 1, 2)
         quantize_w(0, 1, 2)
-        for t in range(TILES):
-            for j in range(PACK):
-                z_pass(0, t, j, 1)
-        cast_w(1, 0, 0)
+        closing(0)
         for t in range(TILES):
             z_round(0, t, nc.scalar.copy)
+        cast_w(1, 0, 0)
+        cast_w(1, 0, 1)
         quantize_w(1, 0, 1)
         for t in range(TILES):
             for j in range(PACK):
                 z_pass(1, t, j, 0)
+        z_quantize(0, 0)
         cast_w(1, 1, 0)
         cast_w(1, 1, 1, 2)
         quantize_w(1, 1, 2)
-        for half in (0, 2):
-            for t in (0, 1):
-                z_pass(1, t, half, 1)
-                z_pass(1, t, half + 1, 1)
-        for t in (2, 3):
-            for j in range(PACK):
-                z_pass(1, t, j, 1)
-        z_quantize(0, 0)
+        closing(1)
+        z_quantize(0, 2)
         z_round(1, 0, nc.scalar.copy)
         z_round(1, 1, nc.vector.tensor_copy)
         z_round(1, 2, nc.scalar.copy)
@@ -227,7 +240,7 @@ def tile_picked_zresc_sig_p_kernel(tc, x_words, x_scales, w1, offs, dst, out):
             z_quantize(1, t)
             y_pass(0, t)
             y_pass(1, t)
-        z_round(1, 3, nc.vector.tensor_copy)
+        z_round(1, 3, nc.scalar.copy)
         for t in (2, 3):
             z_quantize(1, t)
             y_pass(0, t)

@@ -21,10 +21,11 @@ FLOPS = 2 * K * K * S + 2 * K * S * V
 
 CHUNKS = {
     (0, 0): [(0, 128, 56)],
-    (0, 1): [(0, 80, 40), (80, 128, 112)],
-    (1, 0): [(0, 80, 80), (80, 128, 128)],
-    (1, 1): [(0, 80, 64), (80, 128, 116)],
+    (0, 1): [(0, 128, 84)],
+    (1, 0): [(0, 128, 128)],
+    (1, 1): [(0, 128, 88)],
 }
+REUSE = {(1, 0, 0): "table0", (1, 1, 0): "table1"}
 
 
 def tile_picked_zresc_sig_p_kernel(tc, x_words, x_scales, w1, offs, dst, out):
@@ -34,7 +35,7 @@ def tile_picked_zresc_sig_p_kernel(tc, x_words, x_scales, w1, offs, dst, out):
         psum = ctx.enter_context(tc.psum_pool(name="psum", bufs=1))
 
         lists = [keep.tile([P, S // 16], U16, name="offs_sb"), keep.tile([P, V // 16], U16, name="dst_sb")]
-        table = [keep.tile([P, T], I32, name=f"table{g}", align_bytes=64) for g in range(PASSES)]
+        table = {}
         table_scale = keep.tile([P, T], U8, name="table_scale", tag="w_raw010", align_bytes=64)
         picked = [[keep.tile([P, S], U32, name=f"picked{u}{g}", align_bytes=64) for g in range(PASSES)] for u in range(2)]
         staged_scale = keep.tile([P, 2 * S], U8, name="staged_scale", align_bytes=64)
@@ -46,12 +47,10 @@ def tile_picked_zresc_sig_p_kernel(tc, x_words, x_scales, w1, offs, dst, out):
             w_s[b, g] = keep.tile([P, PASS], U8, name=f"w_s{b}{g}", align_bytes=64)
         y_bank = {}
 
-        def load_table(g, pieces):
+        def load_table(g):
             words = x_words[g].rearrange("p n r -> p (n r)").bitcast(I32)
-            width = T // pieces
-            for i in range(pieces):
-                cols = slice(width * i, width * (i + 1))
-                nc.sync.dma_start(out=table[g][:, cols], in_=words[:, cols])
+            table[g] = keep.tile([P, T], I32, name=f"table{g}", tag=f"table{g}", align_bytes=64)
+            nc.sync.dma_start(out=table[g][:], in_=words)
 
         def load_scales():
             for g in range(PASSES):
@@ -62,7 +61,7 @@ def tile_picked_zresc_sig_p_kernel(tc, x_words, x_scales, w1, offs, dst, out):
 
         def place_scales():
             for q in range(4):
-                nc.scalar.dma_start(
+                nc.sync.dma_start(
                     out=planes[32 * q : 32 * q + 8, :].bitcast(I32),
                     in_=staged_scale[q:32:4, :].bitcast(I32),
                 )
@@ -70,11 +69,14 @@ def tile_picked_zresc_sig_p_kernel(tc, x_words, x_scales, w1, offs, dst, out):
         def load_w(b, g):
             rows = w1[PASS * g : PASS * (g + 1), :].rearrange("(p j) c -> p j c", j=PACK)
             for c, (m0, m1, ms) in enumerate(CHUNKS[b, g]):
-                w_raw[b, g, c] = keep.tile([P, PACK, PACK * (m1 - m0)], F32, name=f"w_raw{b}{g}{c}", tag=f"w_raw{b}{g}{c}", align_bytes=64)
+                w_raw[b, g, c] = keep.tile([P, PACK, PACK * (m1 - m0)], F32, name=f"w_raw{b}{g}{c}", tag=REUSE.get((b, g, c), f"w_raw{b}{g}{c}"), align_bytes=64)
                 nc.sync.dma_start(out=w_raw[b, g, c][:], in_=rows[:, :, PASS * b + PACK * m0 : PASS * b + PACK * m1])
 
-        def gather_words(u, g):
-            nc.vector.tensor_copy(picked[u][g][:], table[g][:].bitcast(U32).indirect(lists[u][:]))
+        def gather_words(u, g, pieces=1):
+            width = S // pieces
+            for i in range(pieces):
+                offsets = lists[u][:, width * i // 16 : width * (i + 1) // 16]
+                nc.vector.tensor_copy(picked[u][g][:, width * i : width * (i + 1)], table[g][:].bitcast(U32).indirect(offsets))
 
         def gather_scales(u):
             nc.vector.tensor_copy(staged_scale[:, S * u : S * (u + 1)], table_scale[:].indirect(lists[u][:]))
@@ -175,20 +177,20 @@ def tile_picked_zresc_sig_p_kernel(tc, x_words, x_scales, w1, offs, dst, out):
         load_scales()
         nc.sync.dma_start(lists[0][:], offs)
         nc.sync.dma_start(lists[1][:], dst)
-        load_table(0, 1)
-        load_table(1, 1)
+        load_table(0)
+        load_table(1)
         load_w(0, 0)
         gather_scales(0)
         gather_scales(1)
         place_scales()
         load_w(0, 1)
-        load_w(1, 0)
-        load_w(1, 1)
-
         gather_words(0, 0)
         gather_words(1, 0)
+        load_w(1, 0)
         gather_words(0, 1)
         gather_words(1, 1)
+        load_w(1, 1)
+
         z_bank[1, 0] = psum.tile([P, PACK, P], F32, name="z_bank10", tag="bank10")
         for i in range(6):
             nc.tensor.matmul_mx(
@@ -215,21 +217,18 @@ def tile_picked_zresc_sig_p_kernel(tc, x_words, x_scales, w1, offs, dst, out):
         for t in range(TILES):
             for j in range(PACK):
                 z_pass(0, t, j, 0)
-        cast_w(0, 1, 0)
-        cast_w(0, 1, 1, 2)
+        cast_w(0, 1, 0, 2)
         quantize_w(0, 1, 2)
         closing(0)
         for t in range(TILES):
             z_round(0, t, nc.scalar.copy)
         cast_w(1, 0, 0)
-        cast_w(1, 0, 1)
         quantize_w(1, 0, 1)
         for t in range(TILES):
             for j in range(PACK):
                 z_pass(1, t, j, 0)
         z_quantize(0, 0)
-        cast_w(1, 1, 0)
-        cast_w(1, 1, 1, 2)
+        cast_w(1, 1, 0, 2)
         quantize_w(1, 1, 2)
         closing(1)
         z_quantize(0, 2)

@@ -23,9 +23,9 @@ CHUNKS = {
     (0, 0): [(0, 128, 56)],
     (0, 1): [(0, 128, 84)],
     (1, 0): [(0, 128, 128)],
-    (1, 1): [(0, 128, 88)],
+    (1, 1): [(0, 64, 64), (64, 128, 108)],
 }
-REUSE = {(1, 0, 0): "table0", (1, 1, 0): "table1"}
+REUSE = {(1, 0, 0): "table0", (1, 1, 0): "table1", (1, 1, 1): "w_raw000"}
 
 
 def tile_picked_zresc_sig_p_kernel(tc, x_words, x_scales, w1, offs, dst, out):
@@ -60,7 +60,7 @@ def tile_picked_zresc_sig_p_kernel(tc, x_words, x_scales, w1, offs, dst, out):
                 )
 
         def place_scales():
-            for q in range(4):
+            for q in (0, 2, 1, 3):
                 nc.sync.dma_start(
                     out=planes[32 * q : 32 * q + 8, :].bitcast(I32),
                     in_=staged_scale[q:32:4, :].bitcast(I32),
@@ -135,7 +135,7 @@ def tile_picked_zresc_sig_p_kernel(tc, x_words, x_scales, w1, offs, dst, out):
 
         def z_quantize(b, first):
             count = z_group(b, first)[1]
-            tag = f"w_bf1{first // 2}" if b == 0 else f"z_q{b}{first}"
+            tag = {(0, 0): "w_bf11", (0, 2): "z_bf10"}.get((b, first), f"z_q{b}{first}")
             codes = keep.tile([P, count * P], U32, name=f"z_q{b}{first}", tag=tag, align_bytes=64)
             scales = keep.tile([P, count * P], U8, name=f"z_s{b}{first}", align_bytes=64)
             nc.vector.quantize_mx(
@@ -189,7 +189,6 @@ def tile_picked_zresc_sig_p_kernel(tc, x_words, x_scales, w1, offs, dst, out):
         load_w(1, 0)
         gather_words(0, 1)
         gather_words(1, 1)
-        load_w(1, 1)
 
         z_bank[1, 0] = psum.tile([P, PACK, P], F32, name="z_bank10", tag="bank10")
         for i in range(6):
@@ -217,6 +216,7 @@ def tile_picked_zresc_sig_p_kernel(tc, x_words, x_scales, w1, offs, dst, out):
         for t in range(TILES):
             for j in range(PACK):
                 z_pass(0, t, j, 0)
+        load_w(1, 1)
         cast_w(0, 1, 0, 2)
         quantize_w(0, 1, 2)
         closing(0)
@@ -227,11 +227,11 @@ def tile_picked_zresc_sig_p_kernel(tc, x_words, x_scales, w1, offs, dst, out):
         for t in range(TILES):
             for j in range(PACK):
                 z_pass(1, t, j, 0)
-        z_quantize(0, 0)
-        cast_w(1, 1, 0, 2)
+        cast_w(1, 1, 0)
+        cast_w(1, 1, 1, 2)
         quantize_w(1, 1, 2)
         closing(1)
-        z_quantize(0, 2)
+        z_quantize(0, 0)
         z_round(1, 0, nc.scalar.copy)
         z_round(1, 1, nc.vector.tensor_copy)
         z_round(1, 2, nc.scalar.copy)
@@ -239,6 +239,7 @@ def tile_picked_zresc_sig_p_kernel(tc, x_words, x_scales, w1, offs, dst, out):
             z_quantize(1, t)
             y_pass(0, t)
             y_pass(1, t)
+        z_quantize(0, 2)
         z_round(1, 3, nc.scalar.copy)
         for t in (2, 3):
             z_quantize(1, t)

@@ -109,7 +109,7 @@ def tile_picked_zresc_sig_p_kernel(tc, x_words, x_scales, w1, offs, dst, out):
 
         def z_pass(b, t, j, g):
             if (b, t) not in z_bank:
-                z_bank[b, t] = psum.tile([P, PACK, P], F32, name=f"z_bank{b}{t}", tag=f"bank{b}{t}")
+                z_bank[b, t] = psum.tile([P, PACK, P], F32, name=f"z_bank{b}{t}", tag="bank00" if (b, t) == (0, 3) else f"bank{b}{t}")
             cols = slice(P * j, P * (j + 1))
             toks = slice(P * t, P * (t + 1))
             nc.tensor.matmul_mx(
@@ -149,7 +149,7 @@ def tile_picked_zresc_sig_p_kernel(tc, x_words, x_scales, w1, offs, dst, out):
 
         def y_pass(b, t):
             if t not in y_bank:
-                y_bank[t] = psum.tile([P, V], F32, name=f"y_bank{t}", tag=f"bank0{t}")
+                y_bank[t] = psum.tile([P, V], F32, name=f"y_bank{t}", tag=f"bank0{3 - t}" if t in (0, 3) else f"bank0{t}")
             nc.tensor.matmul_mx(
                 out=y_bank[t][:],
                 lhsT=z_q[b, t].bitcast(FP8X4),
@@ -196,31 +196,35 @@ def tile_picked_zresc_sig_p_kernel(tc, x_words, x_scales, w1, offs, dst, out):
                 out=z_bank[1, 0][:].rearrange("p j n -> p (j n)"),
                 lhsT=picked[0][0][:, 0:P].bitcast(FP8X4),
                 lhsT_scale=staged_scale[:, 0:P],
-                rhs=picked[1][0][:].bitcast(FP8X4),
+                rhs=picked[0][1][:].bitcast(FP8X4),
                 rhs_scale=staged_scale[:, S : 2 * S],
                 start=True,
                 stop=True,
             )
 
-        def closing(b):
+        def closing(b, rest):
             for half in (0, 2):
                 for t in (0, 1):
                     z_pass(b, t, half, 1)
                     z_pass(b, t, half + 1, 1)
-            for t in (2, 3):
+            for t in rest:
                 for j in range(PACK):
                     z_pass(b, t, j, 1)
 
         cast_w(0, 0, 0)
         quantize_w(0, 0, 1)
-        for t in range(TILES):
+        for t in range(TILES - 1):
             for j in range(PACK):
                 z_pass(0, t, j, 0)
         load_w(1, 1)
         cast_w(0, 1, 0, 2)
         quantize_w(0, 1, 2)
-        closing(0)
-        for t in range(TILES):
+        closing(0, (2,))
+        z_round(0, 0, nc.scalar.copy)
+        for g in range(PASSES):
+            for j in range(PACK):
+                z_pass(0, 3, j, g)
+        for t in range(1, TILES):
             z_round(0, t, nc.scalar.copy)
         cast_w(1, 0, 0)
         quantize_w(1, 0, 1)
@@ -230,7 +234,7 @@ def tile_picked_zresc_sig_p_kernel(tc, x_words, x_scales, w1, offs, dst, out):
         cast_w(1, 1, 0)
         cast_w(1, 1, 1, 2)
         quantize_w(1, 1, 2)
-        closing(1)
+        closing(1, (2, 3))
         z_quantize(0, 0)
         z_round(1, 0, nc.scalar.copy)
         z_round(1, 1, nc.vector.tensor_copy)

@@ -22,10 +22,16 @@ FLOPS = 2 * K * K * S + 2 * K * S * V
 CHUNKS = {
     (0, 0): [(0, 128, 56)],
     (0, 1): [(0, 128, 84)],
-    (1, 0): [(0, 128, 128)],
+    (1, 0): [(0, 64, 64), (64, 128, 128)],
     (1, 1): [(0, 64, 64), (64, 128, 108)],
 }
-REUSE = {(1, 0, 0): "table0", (1, 1, 0): "table1", (1, 1, 1): "w_raw000"}
+REUSE = {(1, 0, 0): "table0", (1, 0, 1): "table1", (1, 1, 0): "w_raw000", (1, 1, 1): "w_raw010"}
+PIECES = {
+    0: [("bank03", 0, 256), ("bank10", 256, 512)],
+    1: [("bank01", 0, 512)],
+    2: [("bank02", 0, 512)],
+    3: [("bank00", 0, 512)],
+}
 
 
 def tile_picked_zresc_sig_p_kernel(tc, x_words, x_scales, w1, offs, dst, out):
@@ -135,7 +141,7 @@ def tile_picked_zresc_sig_p_kernel(tc, x_words, x_scales, w1, offs, dst, out):
 
         def z_quantize(b, first):
             count = z_group(b, first)[1]
-            tag = {(0, 0): "w_bf11", (0, 2): "z_bf10"}.get((b, first), f"z_q{b}{first}")
+            tag = {(0, 0): "w_bf10", (0, 2): "w_bf11"}.get((b, first), f"z_q{b}{first}")
             codes = keep.tile([P, count * P], U32, name=f"z_q{b}{first}", tag=tag, align_bytes=64)
             scales = keep.tile([P, count * P], U8, name=f"z_s{b}{first}", align_bytes=64)
             nc.vector.quantize_mx(
@@ -147,26 +153,27 @@ def tile_picked_zresc_sig_p_kernel(tc, x_words, x_scales, w1, offs, dst, out):
                 z_q[b, first + i] = codes[:, P * i : P * (i + 1)]
                 z_s[b, first + i] = scales[:, P * i : P * (i + 1)]
 
-        def y_pass(b, t):
-            if t not in y_bank:
-                y_bank[t] = psum.tile([P, V], F32, name=f"y_bank{t}", tag=f"bank0{3 - t}" if t in (0, 3) else f"bank0{t}")
+        def y_pass(b, t, i=0):
+            tag, c0, c1 = PIECES[t][i]
+            if (t, i) not in y_bank:
+                y_bank[t, i] = psum.tile([P, c1 - c0], F32, name=f"y_bank{t}{i}", tag=tag)
             nc.tensor.matmul_mx(
-                out=y_bank[t][:],
+                out=y_bank[t, i][:],
                 lhsT=z_q[b, t].bitcast(FP8X4),
                 lhsT_scale=z_s[b, t],
-                rhs=picked[1][b][:].bitcast(FP8X4),
-                rhs_scale=planes[4 * b : P, S : 2 * S],
+                rhs=picked[1][b][:, c0:c1].bitcast(FP8X4),
+                rhs_scale=planes[4 * b : P, S + c0 : S + c1],
                 start=(b == 0),
                 stop=(b == PASSES - 1),
             )
 
-        def finish(t, pieces):
-            width = V // pieces
-            for i in range(pieces):
-                cols = slice(width * i, width * (i + 1))
-                result = keep.tile([P, width], F32, name=f"result{t}{i}")
-                nc.scalar.activation(out=result[:], in_=y_bank[t][:, cols], func=SIGMOID)
-                nc.sync.dma_start(out=out[P * t : P * (t + 1), cols], in_=result[:])
+        def finish(t, i, pieces):
+            tag, c0, c1 = PIECES[t][i]
+            width = (c1 - c0) // pieces
+            for h in range(pieces):
+                result = keep.tile([P, width], F32, name=f"result{t}{i}{h}")
+                nc.scalar.activation(out=result[:], in_=y_bank[t, i][:, width * h : width * (h + 1)], func=SIGMOID)
+                nc.sync.dma_start(out=out[P * t : P * (t + 1), c0 + width * h : c0 + width * (h + 1)], in_=result[:])
 
         warm = keep.tile([P, 16], F32, name="warm")
         nc.gpsimd.memset(warm[:, 0:8], 0.0)
@@ -186,9 +193,9 @@ def tile_picked_zresc_sig_p_kernel(tc, x_words, x_scales, w1, offs, dst, out):
         load_w(0, 1)
         gather_words(0, 0)
         gather_words(1, 0)
-        load_w(1, 0)
         gather_words(0, 1)
         gather_words(1, 1)
+        load_w(1, 0)
 
         z_bank[1, 0] = psum.tile([P, PACK, P], F32, name="z_bank10", tag="bank10")
         for i in range(6):
@@ -216,8 +223,8 @@ def tile_picked_zresc_sig_p_kernel(tc, x_words, x_scales, w1, offs, dst, out):
         for t in range(TILES - 1):
             for j in range(PACK):
                 z_pass(0, t, j, 0)
-        load_w(1, 1)
         cast_w(0, 1, 0, 2)
+        load_w(1, 1)
         quantize_w(0, 1, 2)
         closing(0, (2,))
         z_round(0, 0, nc.scalar.copy)
@@ -227,27 +234,33 @@ def tile_picked_zresc_sig_p_kernel(tc, x_words, x_scales, w1, offs, dst, out):
         for t in range(1, TILES):
             z_round(0, t, nc.scalar.copy)
         cast_w(1, 0, 0)
+        cast_w(1, 0, 1)
         quantize_w(1, 0, 1)
         for t in range(TILES):
             for j in range(PACK):
                 z_pass(1, t, j, 0)
+        z_quantize(0, 0)
         cast_w(1, 1, 0)
         cast_w(1, 1, 1, 2)
         quantize_w(1, 1, 2)
         closing(1, (2, 3))
-        z_quantize(0, 0)
+        z_quantize(0, 2)
         z_round(1, 0, nc.scalar.copy)
         z_round(1, 1, nc.vector.tensor_copy)
         z_round(1, 2, nc.scalar.copy)
-        for t in (0, 1):
-            z_quantize(1, t)
-            y_pass(0, t)
-            y_pass(1, t)
-        z_quantize(0, 2)
-        z_round(1, 3, nc.scalar.copy)
+        z_quantize(1, 0)
+        for b in range(PASSES):
+            for i in range(2):
+                y_pass(b, 0, i)
+        z_quantize(1, 1)
+        y_pass(0, 1)
+        y_pass(1, 1)
+        z_round(1, 3, nc.vector.tensor_copy)
         for t in (2, 3):
             z_quantize(1, t)
             y_pass(0, t)
             y_pass(1, t)
-        for t in range(TILES):
-            finish(t, 2 if t == TILES - 1 else 1)
+        finish(0, 0, 1)
+        finish(0, 1, 1)
+        for t in range(1, TILES):
+            finish(t, 0, 2 if t == TILES - 1 else 1)

@@ -197,18 +197,6 @@ def tile_picked_zresc_sig_p_kernel(tc, x_words, x_scales, w1, offs, dst, out):
         gather_words(1, 1)
         load_w(1, 0)
 
-        z_bank[1, 0] = psum.tile([P, PACK, P], F32, name="z_bank10", tag="bank10")
-        for i in range(6):
-            nc.tensor.matmul_mx(
-                out=z_bank[1, 0][:].rearrange("p j n -> p (j n)"),
-                lhsT=picked[0][0][:, 0:P].bitcast(FP8X4),
-                lhsT_scale=staged_scale[:, 0:P],
-                rhs=picked[0][1][:].bitcast(FP8X4),
-                rhs_scale=staged_scale[:, S : 2 * S],
-                start=True,
-                stop=True,
-            )
-
         def closing(b, rest):
             for half in (0, 2):
                 for t in (0, 1):

@@ -25,7 +25,7 @@ CHUNKS = {
     (1, 0): [(0, 64, 64), (64, 128, 128)],
     (1, 1): [(0, 64, 64), (64, 128, 108)],
 }
-REUSE = {(1, 0, 0): "table0", (1, 0, 1): "table1", (1, 1, 0): "w_raw000", (1, 1, 1): "w_raw010"}
+LATER = {(0, 1): 0, (1, 0): 1, (1, 1): 2}
 PIECES = {
     0: [("bank03", 0, 256), ("bank10", 256, 512)],
     1: [("bank01", 0, 512)],
@@ -42,7 +42,7 @@ def tile_picked_zresc_sig_p_kernel(tc, x_words, x_scales, w1, offs, dst, out):
 
         lists = [keep.tile([P, S // 16], U16, name="offs_sb"), keep.tile([P, V // 16], U16, name="dst_sb")]
         table = {}
-        table_scale = keep.tile([P, T], U8, name="table_scale", tag="w_raw010", align_bytes=64)
+        table_scale = keep.tile([P, T], U8, name="table_scale", tag="scale_rows", align_bytes=64)
         picked = [[keep.tile([P, S], U32, name=f"picked{u}{g}", align_bytes=64) for g in range(PASSES)] for u in range(2)]
         staged_scale = keep.tile([P, 2 * S], U8, name="staged_scale", align_bytes=64)
         planes = keep.tile([P, 2 * S], U8, name="planes", align_bytes=64)
@@ -52,6 +52,7 @@ def tile_picked_zresc_sig_p_kernel(tc, x_words, x_scales, w1, offs, dst, out):
             w_q[b, g] = keep.tile([P, PASS], U32, name=f"w_q{b}{g}", align_bytes=64)
             w_s[b, g] = keep.tile([P, PASS], U8, name=f"w_s{b}{g}", align_bytes=64)
         y_bank = {}
+        later = []
 
         def load_table(g):
             words = x_words[g].rearrange("p n r -> p (n r)").bitcast(I32)
@@ -75,8 +76,15 @@ def tile_picked_zresc_sig_p_kernel(tc, x_words, x_scales, w1, offs, dst, out):
         def load_w(b, g):
             rows = w1[PASS * g : PASS * (g + 1), :].rearrange("(p j) c -> p j c", j=PACK)
             for c, (m0, m1, ms) in enumerate(CHUNKS[b, g]):
-                w_raw[b, g, c] = keep.tile([P, PACK, PACK * (m1 - m0)], F32, name=f"w_raw{b}{g}{c}", tag=REUSE.get((b, g, c), f"w_raw{b}{g}{c}"), align_bytes=64)
-                nc.sync.dma_start(out=w_raw[b, g, c][:], in_=rows[:, :, PASS * b + PACK * m0 : PASS * b + PACK * m1])
+                if (b, g) == (0, 0):
+                    first = keep.tile([P, PACK * PASS], F32, name="w_first", align_bytes=64)
+                    w_raw[b, g, c] = first[:].rearrange("p (j c) -> p j c", j=PACK)
+                else:
+                    if not later:
+                        later.append(keep.tile([P, 3 * PACK * PASS], F32, name="w_later", tag="scale_rows", align_bytes=64))
+                    start = PACK * (PASS * LATER[b, g] + PACK * m0)
+                    w_raw[b, g, c] = later[0][:, start : start + PACK * PACK * (m1 - m0)].rearrange("p (j c) -> p j c", j=PACK)
+                nc.sync.dma_start(out=w_raw[b, g, c], in_=rows[:, :, PASS * b + PACK * m0 : PASS * b + PACK * m1])
 
         def gather_words(u, g, pieces=1):
             width = S // pieces
@@ -89,7 +97,7 @@ def tile_picked_zresc_sig_p_kernel(tc, x_words, x_scales, w1, offs, dst, out):
 
         def cast_w(b, g, c, parts=1):
             m0, m1, ms = CHUNKS[b, g][c]
-            src = w_raw[b, g, c][:].rearrange("p j (m e t) -> p m j e t", e=2, t=PACK)
+            src = w_raw[b, g, c].rearrange("p j (m e t) -> p m j e t", e=2, t=PACK)
             dealt = w_bf[b, g][:].rearrange("p t (m e) j -> p m j e t", e=2)
             h0, h1, hs = m0 // 2, m1 // 2, ms // 2
             width = PACK // parts

@@ -22,15 +22,15 @@ FLOPS = 2 * K * K * S + 2 * K * S * V
 CHUNKS = {
     (0, 0): [(0, 128, 56)],
     (0, 1): [(0, 128, 84)],
-    (1, 0): [(0, 64, 64), (64, 128, 128)],
+    (1, 0): [(0, 64, 16), (64, 128, 128)],
     (1, 1): [(0, 64, 64), (64, 128, 108)],
 }
 LATER = {(0, 1): 0, (1, 0): 1, (1, 1): 2}
 PIECES = {
     0: [("bank03", 0, 256), ("bank10", 256, 512)],
     1: [("bank01", 0, 512)],
-    2: [("bank02", 0, 512)],
-    3: [("bank00", 0, 512)],
+    2: [("bank12", 0, 512)],
+    3: [("bank13", 0, 512)],
 }
 
 
@@ -48,7 +48,11 @@ def tile_picked_zresc_sig_p_kernel(tc, x_words, x_scales, w1, offs, dst, out):
         planes = keep.tile([P, 2 * S], U8, name="planes", align_bytes=64)
         w_raw, w_bf, w_q, w_s = {}, {}, {}, {}
         for (b, g), chunks in CHUNKS.items():
-            w_bf[b, g] = keep.tile([P, PACK, P, PACK], BF16, name=f"w_bf{b}{g}", tag=f"w_bf{b}{g}", align_bytes=64)
+            if (b, g) == (1, 1):
+                for c in range(2):
+                    w_bf[b, g, c] = keep.tile([P, PACK, P // 2, PACK], BF16, name=f"w_bf{b}{g}{c}", tag=f"w_bf{b}{g}{c}", align_bytes=64)
+            else:
+                w_bf[b, g] = keep.tile([P, PACK, P, PACK], BF16, name=f"w_bf{b}{g}", tag=f"w_bf{b}{g}", align_bytes=64)
             w_q[b, g] = keep.tile([P, PASS], U32, name=f"w_q{b}{g}", align_bytes=64)
             w_s[b, g] = keep.tile([P, PASS], U8, name=f"w_s{b}{g}", align_bytes=64)
         y_bank = {}
@@ -98,7 +102,11 @@ def tile_picked_zresc_sig_p_kernel(tc, x_words, x_scales, w1, offs, dst, out):
         def cast_w(b, g, c, parts=1):
             m0, m1, ms = CHUNKS[b, g][c]
             src = w_raw[b, g, c].rearrange("p j (m e t) -> p m j e t", e=2, t=PACK)
-            dealt = w_bf[b, g][:].rearrange("p t (m e) j -> p m j e t", e=2)
+            if (b, g) == (1, 1):
+                dealt = w_bf[b, g, c][:].rearrange("p t (m e) j -> p m j e t", e=2)
+                m0, m1, ms = 0, m1 - m0, ms - m0
+            else:
+                dealt = w_bf[b, g][:].rearrange("p t (m e) j -> p m j e t", e=2)
             h0, h1, hs = m0 // 2, m1 // 2, ms // 2
             width = PACK // parts
             for i in range(parts):
@@ -117,6 +125,16 @@ def tile_picked_zresc_sig_p_kernel(tc, x_words, x_scales, w1, offs, dst, out):
                     out=w_q[b, g][:, cols].bitcast(FP8X4),
                     scales=w_s[b, g][:, cols],
                     in_=flat[:, PACK * width * i : PACK * width * (i + 1)],
+                )
+
+        def quantize_half(c):
+            half = P // 2
+            for t in range(PACK):
+                cols = slice(P * t + half * c, P * t + half * (c + 1))
+                nc.vector.quantize_mx(
+                    out=w_q[1, 1][:, cols].bitcast(FP8X4),
+                    scales=w_s[1, 1][:, cols],
+                    in_=w_bf[1, 1, c][:, t].rearrange("p m j -> p (m j)"),
                 )
 
         z_bank, z_bf, z_q, z_s = {}, {}, {}, {}
@@ -139,17 +157,17 @@ def tile_picked_zresc_sig_p_kernel(tc, x_words, x_scales, w1, offs, dst, out):
         def z_round(b, t, engine_copy):
             first, count = z_group(b, t)
             if t == first:
-                tag = f"z_bf{b}{t}"
+                tag = "z_bf11" if (b, t) == (1, 3) else f"z_bf{b}{t}"
                 z_bf[b, first] = keep.tile([P, count * P, PACK], BF16, name=f"z_bf{b}{t}", tag=tag, align_bytes=64)
             toks = slice(P * (t - first), P * (t - first + 1))
             engine_copy(out=z_bf[b, first][:, toks, :], in_=z_bank[b, t][:].rearrange("p j n -> p n j"))
 
         def z_group(b, t):
-            return (t - t % 2, 2) if b == 0 else (t, 1)
+            return (0, TILES) if b == 0 else (t, 1)
 
         def z_quantize(b, first):
             count = z_group(b, first)[1]
-            tag = {(0, 0): "w_bf10", (0, 2): "w_bf11"}.get((b, first), f"z_q{b}{first}")
+            tag = {(0, 0): "w_bf111"}.get((b, first), f"z_q{b}{first}")
             codes = keep.tile([P, count * P], U32, name=f"z_q{b}{first}", tag=tag, align_bytes=64)
             scales = keep.tile([P, count * P], U8, name=f"z_s{b}{first}", align_bytes=64)
             nc.vector.quantize_mx(
@@ -201,6 +219,17 @@ def tile_picked_zresc_sig_p_kernel(tc, x_words, x_scales, w1, offs, dst, out):
         load_w(0, 1)
         gather_words(0, 0)
         gather_words(1, 0)
+        idle = psum.tile([P, V], F32, name="idle", tag="bank13")
+        for i in range(6):
+            nc.tensor.matmul_mx(
+                out=idle[:],
+                lhsT=picked[0][0][:, 0:P].bitcast(FP8X4),
+                lhsT_scale=staged_scale[:, 0:P],
+                rhs=picked[1][0][:].bitcast(FP8X4),
+                rhs_scale=staged_scale[:, S : 2 * S],
+                start=True,
+                stop=True,
+            )
         gather_words(0, 1)
         gather_words(1, 1)
         load_w(1, 0)
@@ -230,17 +259,17 @@ def tile_picked_zresc_sig_p_kernel(tc, x_words, x_scales, w1, offs, dst, out):
         for t in range(1, TILES):
             z_round(0, t, nc.scalar.copy)
         cast_w(1, 0, 0)
-        cast_w(1, 0, 1)
-        quantize_w(1, 0, 1)
+        cast_w(1, 0, 1, 2)
+        quantize_w(1, 0, 2)
         for t in range(TILES):
             for j in range(PACK):
                 z_pass(1, t, j, 0)
-        z_quantize(0, 0)
-        cast_w(1, 1, 0)
+        cast_w(1, 1, 0, 2)
+        quantize_half(0)
         cast_w(1, 1, 1, 2)
-        quantize_w(1, 1, 2)
+        quantize_half(1)
         closing(1, (2, 3))
-        z_quantize(0, 2)
+        z_quantize(0, 0)
         z_round(1, 0, nc.scalar.copy)
         z_round(1, 1, nc.vector.tensor_copy)
         z_round(1, 2, nc.scalar.copy)

@@ -22,12 +22,12 @@ FLOPS = 2 * K * K * S + 2 * K * S * V
 CHUNKS = {
     (0, 0): [(0, 128, 56)],
     (0, 1): [(0, 128, 84)],
-    (1, 0): [(0, 64, 16), (64, 128, 128)],
-    (1, 1): [(0, 64, 64), (64, 128, 108)],
+    (1, 0): [(0, 64, 32), (64, 128, 104)],
+    (1, 1): [(0, 64, 64), (64, 128, 128)],
 }
-LATER = {(0, 1): 0, (1, 0): 1, (1, 1): 2}
+LATER = {(0, 1, 0): 0, (1, 0, 0): 2, (1, 1, 0): 3, (1, 0, 1): 4, (1, 1, 1): 5}
 PIECES = {
-    0: [("bank03", 0, 256), ("bank10", 256, 512)],
+    0: [("bank00", 0, 256), ("bank02", 256, 512)],
     1: [("bank01", 0, 512)],
     2: [("bank12", 0, 512)],
     3: [("bank13", 0, 512)],
@@ -57,6 +57,7 @@ def tile_picked_zresc_sig_p_kernel(tc, x_words, x_scales, w1, offs, dst, out):
             w_s[b, g] = keep.tile([P, PASS], U8, name=f"w_s{b}{g}", align_bytes=64)
         y_bank = {}
         later = []
+        held = []
 
         def load_table(g):
             words = x_words[g].rearrange("p n r -> p (n r)").bitcast(I32)
@@ -86,7 +87,7 @@ def tile_picked_zresc_sig_p_kernel(tc, x_words, x_scales, w1, offs, dst, out):
                 else:
                     if not later:
                         later.append(keep.tile([P, 3 * PACK * PASS], F32, name="w_later", tag="scale_rows", align_bytes=64))
-                    start = PACK * (PASS * LATER[b, g] + PACK * m0)
+                    start = 2 * PASS * LATER[b, g, c]
                     w_raw[b, g, c] = later[0][:, start : start + PACK * PACK * (m1 - m0)].rearrange("p (j c) -> p j c", j=PACK)
                 nc.sync.dma_start(out=w_raw[b, g, c], in_=rows[:, :, PASS * b + PACK * m0 : PASS * b + PACK * m1])
 
@@ -141,7 +142,7 @@ def tile_picked_zresc_sig_p_kernel(tc, x_words, x_scales, w1, offs, dst, out):
 
         def z_pass(b, t, j, g):
             if (b, t) not in z_bank:
-                z_bank[b, t] = psum.tile([P, PACK, P], F32, name=f"z_bank{b}{t}", tag="bank00" if (b, t) == (0, 3) else f"bank{b}{t}")
+                z_bank[b, t] = psum.tile([P, PACK, P], F32, name=f"z_bank{b}{t}", tag=f"bank{b}{t}")
             cols = slice(P * j, P * (j + 1))
             toks = slice(P * t, P * (t + 1))
             nc.tensor.matmul_mx(
@@ -156,9 +157,13 @@ def tile_picked_zresc_sig_p_kernel(tc, x_words, x_scales, w1, offs, dst, out):
 
         def z_round(b, t, engine_copy):
             first, count = z_group(b, t)
-            if t == first:
-                tag = "z_bf11" if (b, t) == (1, 3) else f"z_bf{b}{t}"
-                z_bf[b, first] = keep.tile([P, count * P, PACK], BF16, name=f"z_bf{b}{t}", tag=tag, align_bytes=64)
+            if b == 0:
+                start = 2 * PASS * LATER[1, 0, 1]
+                z_bf[b, first] = later[0][:, start : start + 8 * P].bitcast(BF16).rearrange("p (n j) -> p n j", j=PACK)
+            elif t == first:
+                tag = "z_bf10" if (b, t) == (1, 3) else f"z_bf{b}{t}"
+                own = keep.tile([P, count * P, PACK], BF16, name=f"z_bf{b}{t}", tag=tag, align_bytes=64)
+                z_bf[b, first] = own[:]
             toks = slice(P * (t - first), P * (t - first + 1))
             engine_copy(out=z_bf[b, first][:, toks, :], in_=z_bank[b, t][:].rearrange("p j n -> p n j"))
 
@@ -167,13 +172,18 @@ def tile_picked_zresc_sig_p_kernel(tc, x_words, x_scales, w1, offs, dst, out):
 
         def z_quantize(b, first):
             count = z_group(b, first)[1]
-            tag = {(0, 0): "w_bf111"}.get((b, first), f"z_q{b}{first}")
-            codes = keep.tile([P, count * P], U32, name=f"z_q{b}{first}", tag=tag, align_bytes=64)
+            if b == 0:
+                if first == 0:
+                    held.append(keep.tile([P, S], U32, name="z_q0", tag="w_bf111", align_bytes=64))
+                codes = held[0][:, P * first : P * (first + count)]
+            else:
+                own = keep.tile([P, P], U32, name=f"z_q{b}{first}", align_bytes=64)
+                codes = own[:]
             scales = keep.tile([P, count * P], U8, name=f"z_s{b}{first}", align_bytes=64)
             nc.vector.quantize_mx(
-                out=codes[:].bitcast(FP8X4),
+                out=codes.bitcast(FP8X4),
                 scales=scales[:],
-                in_=z_bf[b, first][:].rearrange("p n j -> p (n j)"),
+                in_=z_bf[b, first].rearrange("p n j -> p (n j)"),
             )
             for i in range(count):
                 z_q[b, first + i] = codes[:, P * i : P * (i + 1)]
@@ -245,21 +255,17 @@ def tile_picked_zresc_sig_p_kernel(tc, x_words, x_scales, w1, offs, dst, out):
 
         cast_w(0, 0, 0)
         quantize_w(0, 0, 1)
-        for t in range(TILES - 1):
+        for t in range(TILES):
             for j in range(PACK):
                 z_pass(0, t, j, 0)
         cast_w(0, 1, 0, 2)
         load_w(1, 1)
         quantize_w(0, 1, 2)
-        closing(0, (2,))
-        z_round(0, 0, nc.scalar.copy)
-        for g in range(PASSES):
-            for j in range(PACK):
-                z_pass(0, 3, j, g)
-        for t in range(1, TILES):
-            z_round(0, t, nc.scalar.copy)
+        closing(0, (2, 3))
         cast_w(1, 0, 0)
         cast_w(1, 0, 1, 2)
+        for t in range(TILES):
+            z_round(0, t, nc.scalar.copy)
         quantize_w(1, 0, 2)
         for t in range(TILES):
             for j in range(PACK):

@@ -22,7 +22,7 @@ FLOPS = 2 * K * K * S + 2 * K * S * V
 CHUNKS = {
     (0, 0): [(0, 128, 56)],
     (0, 1): [(0, 128, 84)],
-    (1, 0): [(0, 64, 32), (64, 128, 104)],
+    (1, 0): [(0, 64, 16), (64, 128, 104)],
     (1, 1): [(0, 64, 64), (64, 128, 128)],
 }
 LATER = {(0, 1, 0): 0, (1, 0, 0): 2, (1, 1, 0): 3, (1, 0, 1): 4, (1, 1, 1): 5}
@@ -294,4 +294,4 @@ def tile_picked_zresc_sig_p_kernel(tc, x_words, x_scales, w1, offs, dst, out):
         finish(0, 0, 1)
         finish(0, 1, 1)
         for t in range(1, TILES):
-            finish(t, 0, 2 if t == TILES - 1 else 1)
+            finish(t, 0, 2)

@@ -229,17 +229,6 @@ def tile_picked_zresc_sig_p_kernel(tc, x_words, x_scales, w1, offs, dst, out):
         load_w(0, 1)
         gather_words(0, 0)
         gather_words(1, 0)
-        idle = psum.tile([P, V], F32, name="idle", tag="bank13")
-        for i in range(6):
-            nc.tensor.matmul_mx(
-                out=idle[:],
-                lhsT=picked[0][0][:, 0:P].bitcast(FP8X4),
-                lhsT_scale=staged_scale[:, 0:P],
-                rhs=picked[1][0][:].bitcast(FP8X4),
-                rhs_scale=staged_scale[:, S : 2 * S],
-                start=True,
-                stop=True,
-            )
         gather_words(0, 1)
         gather_words(1, 1)
         load_w(1, 0)

@@ -140,7 +140,7 @@ def tile_picked_zresc_sig_p_kernel(tc, x_words, x_scales, w1, offs, dst, out):
 
         z_bank, z_bf, z_q, z_s = {}, {}, {}, {}
 
-        def z_pass(b, t, j, g):
+        def z_pass(b, t, j, g, ends=((0, 0), (PACK - 1, PASSES - 1))):
             if (b, t) not in z_bank:
                 z_bank[b, t] = psum.tile([P, PACK, P], F32, name=f"z_bank{b}{t}", tag=f"bank{b}{t}")
             cols = slice(P * j, P * (j + 1))
@@ -151,8 +151,8 @@ def tile_picked_zresc_sig_p_kernel(tc, x_words, x_scales, w1, offs, dst, out):
                 lhsT_scale=w_s[b, g][:, cols],
                 rhs=picked[0][g][:, toks].bitcast(FP8X4),
                 rhs_scale=planes[4 * g : P, toks],
-                start=(g == 0 and j == 0),
-                stop=(g == PASSES - 1 and j == PACK - 1),
+                start=((j, g) == ends[0]),
+                stop=((j, g) == ends[1]),
             )
 
         def z_round(b, t, engine_copy):
@@ -244,13 +244,17 @@ def tile_picked_zresc_sig_p_kernel(tc, x_words, x_scales, w1, offs, dst, out):
 
         cast_w(0, 0, 0)
         quantize_w(0, 0, 1)
-        for t in range(TILES):
+        for t in range(2):
             for j in range(PACK):
                 z_pass(0, t, j, 0)
         cast_w(0, 1, 0, 2)
         load_w(1, 1)
         quantize_w(0, 1, 2)
-        closing(0, (2, 3))
+        closing(0, ())
+        for t in (2, 3):
+            for g in reversed(range(PASSES)):
+                for j in reversed(range(PACK)):
+                    z_pass(0, t, j, g, ((PACK - 1, PASSES - 1), (0, 0)))
         cast_w(1, 0, 0)
         cast_w(1, 0, 1, 2)
         for t in range(TILES):

@@ -22,7 +22,7 @@ FLOPS = 2 * K * K * S + 2 * K * S * V
 CHUNKS = {
     (0, 0): [(0, 128, 56)],
     (0, 1): [(0, 128, 84)],
-    (1, 0): [(0, 64, 16), (64, 128, 104)],
+    (1, 0): [(0, 64, 32), (64, 128, 104)],
     (1, 1): [(0, 64, 64), (64, 128, 128)],
 }
 LATER = {(0, 1, 0): 0, (1, 0, 0): 2, (1, 1, 0): 3, (1, 0, 1): 4, (1, 1, 1): 5}
@@ -48,7 +48,7 @@ def tile_picked_zresc_sig_p_kernel(tc, x_words, x_scales, w1, offs, dst, out):
         planes = keep.tile([P, 2 * S], U8, name="planes", align_bytes=64)
         w_raw, w_bf, w_q, w_s = {}, {}, {}, {}
         for (b, g), chunks in CHUNKS.items():
-            if (b, g) == (1, 1):
+            if b == 1:
                 for c in range(2):
                     w_bf[b, g, c] = keep.tile([P, PACK, P // 2, PACK], BF16, name=f"w_bf{b}{g}{c}", tag=f"w_bf{b}{g}{c}", align_bytes=64)
             else:
@@ -103,7 +103,7 @@ def tile_picked_zresc_sig_p_kernel(tc, x_words, x_scales, w1, offs, dst, out):
         def cast_w(b, g, c, parts=1):
             m0, m1, ms = CHUNKS[b, g][c]
             src = w_raw[b, g, c].rearrange("p j (m e t) -> p m j e t", e=2, t=PACK)
-            if (b, g) == (1, 1):
+            if b == 1:
                 dealt = w_bf[b, g, c][:].rearrange("p t (m e) j -> p m j e t", e=2)
                 m0, m1, ms = 0, m1 - m0, ms - m0
             else:
@@ -128,14 +128,14 @@ def tile_picked_zresc_sig_p_kernel(tc, x_words, x_scales, w1, offs, dst, out):
                     in_=flat[:, PACK * width * i : PACK * width * (i + 1)],
                 )
 
-        def quantize_half(c):
+        def quantize_half(g, c):
             half = P // 2
             for t in range(PACK):
                 cols = slice(P * t + half * c, P * t + half * (c + 1))
                 nc.vector.quantize_mx(
-                    out=w_q[1, 1][:, cols].bitcast(FP8X4),
-                    scales=w_s[1, 1][:, cols],
-                    in_=w_bf[1, 1, c][:, t].rearrange("p m j -> p (m j)"),
+                    out=w_q[1, g][:, cols].bitcast(FP8X4),
+                    scales=w_s[1, g][:, cols],
+                    in_=w_bf[1, g, c][:, t].rearrange("p m j -> p (m j)"),
                 )
 
         z_bank, z_bf, z_q, z_s = {}, {}, {}, {}
@@ -255,18 +255,19 @@ def tile_picked_zresc_sig_p_kernel(tc, x_words, x_scales, w1, offs, dst, out):
             for g in reversed(range(PASSES)):
                 for j in reversed(range(PACK)):
                     z_pass(0, t, j, g, ((PACK - 1, PASSES - 1), (0, 0)))
-        cast_w(1, 0, 0)
+        cast_w(1, 0, 0, 2)
+        quantize_half(0, 0)
         cast_w(1, 0, 1, 2)
         for t in range(TILES):
             z_round(0, t, nc.scalar.copy)
-        quantize_w(1, 0, 2)
+        quantize_half(0, 1)
         for t in range(TILES):
             for j in range(PACK):
                 z_pass(1, t, j, 0)
         cast_w(1, 1, 0, 2)
-        quantize_half(0)
+        quantize_half(1, 0)
         cast_w(1, 1, 1, 2)
-        quantize_half(1)
+        quantize_half(1, 1)
         closing(1, (2, 3))
         z_quantize(0, 0)
         z_round(1, 0, nc.scalar.copy)

@@ -40,28 +40,28 @@ def tile_picked_zresc_sig_p_kernel(tc, x_words, x_scales, w1, offs, dst, out):
         keep = ctx.enter_context(tc.tile_pool(name="keep", bufs=1))
         psum = ctx.enter_context(tc.psum_pool(name="psum", bufs=1))
 
-        lists = [keep.tile([P, S // 16], U16, name="offs_sb"), keep.tile([P, V // 16], U16, name="dst_sb")]
+        lists = [keep.tile([P, S // 16], U16, name="offs_sb", align_bytes=256), keep.tile([P, V // 16], U16, name="dst_sb", align_bytes=256)]
         table = {}
-        table_scale = keep.tile([P, T], U8, name="table_scale", tag="scale_rows", align_bytes=64)
-        picked = [[keep.tile([P, S], U32, name=f"picked{u}{g}", align_bytes=64) for g in range(PASSES)] for u in range(2)]
-        staged_scale = keep.tile([P, 2 * S], U8, name="staged_scale", align_bytes=64)
-        planes = keep.tile([P, 2 * S], U8, name="planes", align_bytes=64)
+        table_scale = keep.tile([P, T], U8, name="table_scale", tag="scale_rows", align_bytes=256)
+        picked = [[keep.tile([P, S], U32, name=f"picked{u}{g}", align_bytes=256) for g in range(PASSES)] for u in range(2)]
+        staged_scale = keep.tile([P, 2 * S], U8, name="staged_scale", align_bytes=256)
+        planes = keep.tile([P, 2 * S], U8, name="planes", align_bytes=256)
         w_raw, w_bf, w_q, w_s = {}, {}, {}, {}
         for (b, g), chunks in CHUNKS.items():
             if b == 1:
                 for c in range(2):
-                    w_bf[b, g, c] = keep.tile([P, PACK, P // 2, PACK], BF16, name=f"w_bf{b}{g}{c}", tag=f"w_bf{b}{g}{c}", align_bytes=64)
+                    w_bf[b, g, c] = keep.tile([P, PACK, P // 2, PACK], BF16, name=f"w_bf{b}{g}{c}", tag=f"w_bf{b}{g}{c}", align_bytes=256)
             else:
-                w_bf[b, g] = keep.tile([P, PACK, P, PACK], BF16, name=f"w_bf{b}{g}", tag=f"w_bf{b}{g}", align_bytes=64)
-            w_q[b, g] = keep.tile([P, PASS], U32, name=f"w_q{b}{g}", align_bytes=64)
-            w_s[b, g] = keep.tile([P, PASS], U8, name=f"w_s{b}{g}", align_bytes=64)
+                w_bf[b, g] = keep.tile([P, PACK, P, PACK], BF16, name=f"w_bf{b}{g}", tag=f"w_bf{b}{g}", align_bytes=256)
+            w_q[b, g] = keep.tile([P, PASS], U32, name=f"w_q{b}{g}", align_bytes=256)
+            w_s[b, g] = keep.tile([P, PASS], U8, name=f"w_s{b}{g}", align_bytes=256)
         y_bank = {}
         later = []
         held = []
 
         def load_table(g):
             words = x_words[g].rearrange("p n r -> p (n r)").bitcast(I32)
-            table[g] = keep.tile([P, T], I32, name=f"table{g}", tag=f"table{g}", align_bytes=64)
+            table[g] = keep.tile([P, T], I32, name=f"table{g}", tag=f"table{g}", align_bytes=256)
             nc.sync.dma_start(out=table[g][:], in_=words)
 
         def load_scales():
@@ -82,11 +82,11 @@ def tile_picked_zresc_sig_p_kernel(tc, x_words, x_scales, w1, offs, dst, out):
             rows = w1[PASS * g : PASS * (g + 1), :].rearrange("(p j) c -> p j c", j=PACK)
             for c, (m0, m1, ms) in enumerate(CHUNKS[b, g]):
                 if (b, g) == (0, 0):
-                    first = keep.tile([P, PACK * PASS], F32, name="w_first", align_bytes=64)
+                    first = keep.tile([P, PACK * PASS], F32, name="w_first", align_bytes=256)
                     w_raw[b, g, c] = first[:].rearrange("p (j c) -> p j c", j=PACK)
                 else:
                     if not later:
-                        later.append(keep.tile([P, 3 * PACK * PASS], F32, name="w_later", tag="scale_rows", align_bytes=64))
+                        later.append(keep.tile([P, 3 * PACK * PASS], F32, name="w_later", tag="scale_rows", align_bytes=256))
                     start = 2 * PASS * LATER[b, g, c]
                     w_raw[b, g, c] = later[0][:, start : start + PACK * PACK * (m1 - m0)].rearrange("p (j c) -> p j c", j=PACK)
                 nc.sync.dma_start(out=w_raw[b, g, c], in_=rows[:, :, PASS * b + PACK * m0 : PASS * b + PACK * m1])
@@ -162,7 +162,7 @@ def tile_picked_zresc_sig_p_kernel(tc, x_words, x_scales, w1, offs, dst, out):
                 z_bf[b, first] = later[0][:, start : start + 8 * P].bitcast(BF16).rearrange("p (n j) -> p n j", j=PACK)
             elif t == first:
                 tag = "z_bf10" if (b, t) == (1, 3) else f"z_bf{b}{t}"
-                own = keep.tile([P, count * P, PACK], BF16, name=f"z_bf{b}{t}", tag=tag, align_bytes=64)
+                own = keep.tile([P, count * P, PACK], BF16, name=f"z_bf{b}{t}", tag=tag, align_bytes=256)
                 z_bf[b, first] = own[:]
             toks = slice(P * (t - first), P * (t - first + 1))
             engine_copy(out=z_bf[b, first][:, toks, :], in_=z_bank[b, t][:].rearrange("p j n -> p n j"))
@@ -174,12 +174,12 @@ def tile_picked_zresc_sig_p_kernel(tc, x_words, x_scales, w1, offs, dst, out):
             count = z_group(b, first)[1]
             if b == 0:
                 if first == 0:
-                    held.append(keep.tile([P, S], U32, name="z_q0", tag="w_bf111", align_bytes=64))
+                    held.append(keep.tile([P, S], U32, name="z_q0", tag="w_bf111", align_bytes=256))
                 codes = held[0][:, P * first : P * (first + count)]
             else:
-                own = keep.tile([P, P], U32, name=f"z_q{b}{first}", align_bytes=64)
+                own = keep.tile([P, P], U32, name=f"z_q{b}{first}", align_bytes=256)
                 codes = own[:]
-            scales = keep.tile([P, count * P], U8, name=f"z_s{b}{first}", align_bytes=64)
+            scales = keep.tile([P, count * P], U8, name=f"z_s{b}{first}", align_bytes=256)
             nc.vector.quantize_mx(
                 out=codes.bitcast(FP8X4),
                 scales=scales[:],
@@ -207,7 +207,7 @@ def tile_picked_zresc_sig_p_kernel(tc, x_words, x_scales, w1, offs, dst, out):
             tag, c0, c1 = PIECES[t][i]
             width = (c1 - c0) // pieces
             for h in range(pieces):
-                result = keep.tile([P, width], F32, name=f"result{t}{i}{h}")
+                result = keep.tile([P, width], F32, name=f"result{t}{i}{h}", align_bytes=256)
                 nc.scalar.activation(out=result[:], in_=y_bank[t, i][:, width * h : width * (h + 1)], func=SIGMOID)
                 nc.sync.dma_start(out=out[P * t : P * (t + 1), c0 + width * h : c0 + width * (h + 1)], in_=result[:])
 

@@ -45,7 +45,7 @@ def tile_picked_zresc_sig_p_kernel(tc, x_words, x_scales, w1, offs, dst, out):
         table_scale = keep.tile([P, T], U8, name="table_scale", tag="scale_rows", align_bytes=256)
         picked = [[keep.tile([P, S], U32, name=f"picked{u}{g}", align_bytes=256) for g in range(PASSES)] for u in range(2)]
         staged_scale = keep.tile([P, 2 * S], U8, name="staged_scale", align_bytes=256)
-        planes = keep.tile([P, 2 * S], U8, name="planes", align_bytes=256)
+        planes = [keep.tile([P, 2 * S], U8, name=f"planes{g}", align_bytes=256) for g in range(PASSES)]
         w_raw, w_bf, w_q, w_s = {}, {}, {}, {}
         for (b, g), chunks in CHUNKS.items():
             if b == 1:
@@ -65,17 +65,13 @@ def tile_picked_zresc_sig_p_kernel(tc, x_words, x_scales, w1, offs, dst, out):
             nc.sync.dma_start(out=table[g][:], in_=words)
 
         def load_scales():
-            for g in range(PASSES):
-                nc.sync.dma_start(
-                    out=table_scale[16 * g : 16 * (g + 1), :].bitcast(I32),
-                    in_=x_scales[g].bitcast(I32).rearrange("(q r) n -> r q n", r=4),
-                )
+            nc.sync.dma_start(out=table_scale[0:32, :].bitcast(I32), in_=x_scales.rearrange("g q n -> (g q) n").bitcast(I32))
 
-        def place_scales():
+        def place_scales(g):
             for q in (0, 2, 1, 3):
                 nc.sync.dma_start(
-                    out=planes[32 * q : 32 * q + 8, :].bitcast(I32),
-                    in_=staged_scale[q:32:4, :].bitcast(I32),
+                    out=planes[g][32 * q + 4 * g : 32 * q + 4 * g + 4, :].bitcast(I32),
+                    in_=staged_scale[16 * g + 4 * q : 16 * g + 4 * q + 4, :].bitcast(I32),
                 )
 
         def load_w(b, g):
@@ -150,7 +146,7 @@ def tile_picked_zresc_sig_p_kernel(tc, x_words, x_scales, w1, offs, dst, out):
                 lhsT=w_q[b, g][:, cols].bitcast(FP8X4),
                 lhsT_scale=w_s[b, g][:, cols],
                 rhs=picked[0][g][:, toks].bitcast(FP8X4),
-                rhs_scale=planes[4 * g : P, toks],
+                rhs_scale=planes[g][4 * g : P, toks],
                 start=((j, g) == ends[0]),
                 stop=((j, g) == ends[1]),
             )
@@ -198,7 +194,7 @@ def tile_picked_zresc_sig_p_kernel(tc, x_words, x_scales, w1, offs, dst, out):
                 lhsT=z_q[b, t].bitcast(FP8X4),
                 lhsT_scale=z_s[b, t],
                 rhs=picked[1][b][:, c0:c1].bitcast(FP8X4),
-                rhs_scale=planes[4 * b : P, S + c0 : S + c1],
+                rhs_scale=planes[b][4 * b : P, S + c0 : S + c1],
                 start=(b == 0),
                 stop=(b == PASSES - 1),
             )
@@ -216,7 +212,8 @@ def tile_picked_zresc_sig_p_kernel(tc, x_words, x_scales, w1, offs, dst, out):
         nc.scalar.activation(out=warm[:, 8:16], in_=warm[:, 0:8], func=SIGMOID)
         nc.vector.memset(table_scale[32:64, :].bitcast(I32), 0)
         nc.vector.memset(table_scale[64:P, :].bitcast(I32), 0)
-        nc.vector.memset(planes[:].bitcast(I32), 0)
+        for g in range(PASSES):
+            nc.vector.memset(planes[g][:].bitcast(I32), 0)
         load_scales()
         nc.sync.dma_start(lists[0][:], offs)
         nc.sync.dma_start(lists[1][:], dst)
@@ -225,8 +222,9 @@ def tile_picked_zresc_sig_p_kernel(tc, x_words, x_scales, w1, offs, dst, out):
         load_w(0, 0)
         gather_scales(0)
         gather_scales(1)
-        place_scales()
+        place_scales(0)
         load_w(0, 1)
+        place_scales(1)
         gather_words(0, 0)
         gather_words(1, 0)
         gather_words(0, 1)

@@ -45,7 +45,8 @@ def tile_picked_zresc_sig_p_kernel(tc, x_words, x_scales, w1, offs, dst, out):
         table_scale = keep.tile([P, T], U8, name="table_scale", tag="scale_rows", align_bytes=256)
         picked = [[keep.tile([P, S], U32, name=f"picked{u}{g}", align_bytes=256) for g in range(PASSES)] for u in range(2)]
         staged_scale = keep.tile([P, 2 * S], U8, name="staged_scale", align_bytes=256)
-        planes = [keep.tile([P, 2 * S], U8, name=f"planes{g}", align_bytes=256) for g in range(PASSES)]
+        planes = keep.tile([P, 2 * S], U8, name="planes", align_bytes=256)
+        last_plane = keep.tile([P, V], U8, name="last_plane", align_bytes=256)
         w_raw, w_bf, w_q, w_s = {}, {}, {}, {}
         for (b, g), chunks in CHUNKS.items():
             if b == 1:
@@ -67,12 +68,16 @@ def tile_picked_zresc_sig_p_kernel(tc, x_words, x_scales, w1, offs, dst, out):
         def load_scales():
             nc.sync.dma_start(out=table_scale[0:32, :].bitcast(I32), in_=x_scales.rearrange("g q n -> (g q) n").bitcast(I32))
 
-        def place_scales(g):
-            for q in (0, 2, 1, 3):
-                nc.sync.dma_start(
-                    out=planes[g][32 * q + 4 * g : 32 * q + 4 * g + 4, :].bitcast(I32),
-                    in_=staged_scale[16 * g + 4 * q : 16 * g + 4 * q + 4, :].bitcast(I32),
-                )
+        def place_rows(q, g, c0, c1):
+            nc.sync.dma_start(
+                out=planes[32 * q + 4 * g : 32 * q + 4 * g + 4, c0:c1].bitcast(I32),
+                in_=staged_scale[16 * g + 4 * q : 16 * g + 4 * q + 4, c0:c1].bitcast(I32),
+            )
+
+        def place_scales(quadrants):
+            for q in quadrants:
+                place_rows(q, 0, 0, 2 * S)
+                place_rows(q, 1, 0, S)
 
         def load_w(b, g):
             rows = w1[PASS * g : PASS * (g + 1), :].rearrange("(p j) c -> p j c", j=PACK)
@@ -146,7 +151,7 @@ def tile_picked_zresc_sig_p_kernel(tc, x_words, x_scales, w1, offs, dst, out):
                 lhsT=w_q[b, g][:, cols].bitcast(FP8X4),
                 lhsT_scale=w_s[b, g][:, cols],
                 rhs=picked[0][g][:, toks].bitcast(FP8X4),
-                rhs_scale=planes[g][4 * g : P, toks],
+                rhs_scale=planes[4 * g : P, toks],
                 start=((j, g) == ends[0]),
                 stop=((j, g) == ends[1]),
             )
@@ -194,7 +199,7 @@ def tile_picked_zresc_sig_p_kernel(tc, x_words, x_scales, w1, offs, dst, out):
                 lhsT=z_q[b, t].bitcast(FP8X4),
                 lhsT_scale=z_s[b, t],
                 rhs=picked[1][b][:, c0:c1].bitcast(FP8X4),
-                rhs_scale=planes[b][4 * b : P, S + c0 : S + c1],
+                rhs_scale=planes[:, S + c0 : S + c1] if b == 0 else last_plane[:, c0:c1],
                 start=(b == 0),
                 stop=(b == PASSES - 1),
             )
@@ -212,8 +217,8 @@ def tile_picked_zresc_sig_p_kernel(tc, x_words, x_scales, w1, offs, dst, out):
         nc.scalar.activation(out=warm[:, 8:16], in_=warm[:, 0:8], func=SIGMOID)
         nc.vector.memset(table_scale[32:64, :].bitcast(I32), 0)
         nc.vector.memset(table_scale[64:P, :].bitcast(I32), 0)
-        for g in range(PASSES):
-            nc.vector.memset(planes[g][:].bitcast(I32), 0)
+        nc.vector.memset(planes[:].bitcast(I32), 0)
+        nc.vector.memset(last_plane[:].bitcast(I32), 0)
         load_scales()
         nc.sync.dma_start(lists[0][:], offs)
         nc.sync.dma_start(lists[1][:], dst)
@@ -222,9 +227,9 @@ def tile_picked_zresc_sig_p_kernel(tc, x_words, x_scales, w1, offs, dst, out):
         load_w(0, 0)
         gather_scales(0)
         gather_scales(1)
-        place_scales(0)
+        place_scales((0, 2))
         load_w(0, 1)
-        place_scales(1)
+        place_scales((1, 3))
         gather_words(0, 0)
         gather_words(1, 0)
         gather_words(0, 1)
@@ -247,6 +252,8 @@ def tile_picked_zresc_sig_p_kernel(tc, x_words, x_scales, w1, offs, dst, out):
                 z_pass(0, t, j, 0)
         cast_w(0, 1, 0, 2)
         load_w(1, 1)
+        for q in (0, 2, 1, 3):
+            nc.sync.dma_start(out=last_plane[32 * q : 32 * q + 4, :].bitcast(I32), in_=staged_scale[16 + 4 * q : 20 + 4 * q, S : 2 * S].bitcast(I32))
         quantize_w(0, 1, 2)
         closing(0, ())
         for t in (2, 3):

@@ -17,20 +17,25 @@ PASS = P * PACK
 K, T, S, V = 1024, 2048, 512, 512
 PASSES = K // PASS
 TILES = S // P
+HALF = P // 2
+ROWS = 4
+ALIGN = 256
+ROW_ALIGN = 2048
 FLOPS = 2 * K * K * S + 2 * K * S * V
 
-CHUNKS = {
+LOADS = {
     (0, 0): [(0, 128, 56)],
     (0, 1): [(0, 128, 84)],
     (1, 0): [(0, 64, 32), (64, 128, 104)],
     (1, 1): [(0, 64, 64), (64, 128, 128)],
 }
-LATER = {(0, 1, 0): 0, (1, 0, 0): 2, (1, 1, 0): 3, (1, 0, 1): 4, (1, 1, 1): 5}
-PIECES = {
-    0: [("bank00", 0, 256), ("bank02", 256, 512)],
-    1: [("bank01", 0, 512)],
-    2: [("bank12", 0, 512)],
-    3: [("bank13", 0, 512)],
+PLACE = {(0, 1, 0): 0, (1, 0, 0): 2, (1, 1, 0): 3, (1, 0, 1): 4, (1, 1, 1): 5}
+HALF_PART = PACK * PASS // 2
+Y_BANKS = {
+    0: [("bank00", 0, V // 2), ("bank02", V // 2, V)],
+    1: [("bank01", 0, V)],
+    2: [("bank12", 0, V)],
+    3: [("bank13", 0, V)],
 }
 
 
@@ -38,110 +43,83 @@ def tile_picked_zresc_sig_p_kernel(tc, x_words, x_scales, w1, offs, dst, out):
     nc = tc.nc
     with ExitStack() as ctx:
         keep = ctx.enter_context(tc.tile_pool(name="keep", bufs=1))
+        wide = ctx.enter_context(tc.tile_pool(name="wide", bufs=1))
         psum = ctx.enter_context(tc.psum_pool(name="psum", bufs=1))
 
-        lists = [keep.tile([P, S // 16], U16, name="offs_sb", align_bytes=256), keep.tile([P, V // 16], U16, name="dst_sb", align_bytes=256)]
-        table = {}
-        table_scale = keep.tile([P, T], U8, name="table_scale", tag="scale_rows", align_bytes=256)
-        picked = [[keep.tile([P, S], U32, name=f"picked{u}{g}", align_bytes=256) for g in range(PASSES)] for u in range(2)]
-        staged_scale = keep.tile([P, 2 * S], U8, name="staged_scale", align_bytes=256)
-        planes = keep.tile([P, 2 * S], U8, name="planes", align_bytes=256)
-        last_plane = keep.tile([P, V], U8, name="last_plane", align_bytes=256)
-        w_raw, w_bf, w_q, w_s = {}, {}, {}, {}
-        for (b, g), chunks in CHUNKS.items():
-            if b == 1:
-                for c in range(2):
-                    w_bf[b, g, c] = keep.tile([P, PACK, P // 2, PACK], BF16, name=f"w_bf{b}{g}{c}", tag=f"w_bf{b}{g}{c}", align_bytes=256)
-            else:
-                w_bf[b, g] = keep.tile([P, PACK, P, PACK], BF16, name=f"w_bf{b}{g}", tag=f"w_bf{b}{g}", align_bytes=256)
-            w_q[b, g] = keep.tile([P, PASS], U32, name=f"w_q{b}{g}", align_bytes=256)
-            w_s[b, g] = keep.tile([P, PASS], U8, name=f"w_s{b}{g}", align_bytes=256)
-        y_bank = {}
-        later = []
-        held = []
+        lists = [
+            keep.tile([P, S // 16], U16, name="offs_sb", align_bytes=ALIGN),
+            keep.tile([P, V // 16], U16, name="dst_sb", align_bytes=ALIGN),
+        ]
+        table_scale = wide.tile([P, T], U8, name="table_scale", tag="scale_rows", align_bytes=ROW_ALIGN)
+        picked = [[keep.tile([P, S], U32, name=f"picked{u}{g}", align_bytes=ALIGN) for g in range(PASSES)] for u in range(2)]
+        picked_scale = keep.tile([P, S + V], U8, name="picked_scale", align_bytes=ALIGN)
+        planes = keep.tile([P, S + V], U8, name="planes", align_bytes=ALIGN)
+        last_plane = keep.tile([P, V], U8, name="last_plane", align_bytes=ALIGN)
+        w_bf, w_q, w_s = {}, {}, {}
+        for (b, g), loads in LOADS.items():
+            for c, (m0, m1, ms) in enumerate(loads):
+                name = f"w_bf{b}{g}{c}"
+                w_bf[b, g, c] = keep.tile([P, PACK, m1 - m0, PACK], BF16, name=name, tag=name, align_bytes=ALIGN)
+            w_q[b, g] = keep.tile([P, PASS], U32, name=f"w_q{b}{g}", align_bytes=ALIGN)
+            w_s[b, g] = keep.tile([P, PASS], U8, name=f"w_s{b}{g}", align_bytes=ALIGN)
+        table, w_raw, z_bank, z_bf, z_q, z_s, y_bank = {}, {}, {}, {}, {}, {}, {}
 
         def load_table(g):
-            words = x_words[g].rearrange("p n r -> p (n r)").bitcast(I32)
-            table[g] = keep.tile([P, T], I32, name=f"table{g}", tag=f"table{g}", align_bytes=256)
-            nc.sync.dma_start(out=table[g][:], in_=words)
+            table[g] = wide.tile([P, T], I32, name=f"table{g}", align_bytes=ROW_ALIGN)
+            nc.sync.dma_start(out=table[g][:], in_=x_words[g].rearrange("p n r -> p (n r)").bitcast(I32))
 
-        def load_scales():
-            nc.sync.dma_start(out=table_scale[0:32, :].bitcast(I32), in_=x_scales.rearrange("g q n -> (g q) n").bitcast(I32))
-
-        def place_rows(q, g, c0, c1):
-            nc.sync.dma_start(
-                out=planes[32 * q + 4 * g : 32 * q + 4 * g + 4, c0:c1].bitcast(I32),
-                in_=staged_scale[16 * g + 4 * q : 16 * g + 4 * q + 4, c0:c1].bitcast(I32),
-            )
-
-        def place_scales(quadrants):
-            for q in quadrants:
-                place_rows(q, 0, 0, 2 * S)
-                place_rows(q, 1, 0, S)
-
-        def load_w(b, g):
+        def load_w(b, g, tile, places):
             rows = w1[PASS * g : PASS * (g + 1), :].rearrange("(p j) c -> p j c", j=PACK)
-            for c, (m0, m1, ms) in enumerate(CHUNKS[b, g]):
-                if (b, g) == (0, 0):
-                    first = keep.tile([P, PACK * PASS], F32, name="w_first", align_bytes=256)
-                    w_raw[b, g, c] = first[:].rearrange("p (j c) -> p j c", j=PACK)
-                else:
-                    if not later:
-                        later.append(keep.tile([P, 3 * PACK * PASS], F32, name="w_later", tag="scale_rows", align_bytes=256))
-                    start = 2 * PASS * LATER[b, g, c]
-                    w_raw[b, g, c] = later[0][:, start : start + PACK * PACK * (m1 - m0)].rearrange("p (j c) -> p j c", j=PACK)
+            for c, (m0, m1, ms) in enumerate(LOADS[b, g]):
+                start = HALF_PART * places[c]
+                w_raw[b, g, c] = tile[:, start : start + PACK * PACK * (m1 - m0)].rearrange("p (j c) -> p j c", j=PACK)
                 nc.sync.dma_start(out=w_raw[b, g, c], in_=rows[:, :, PASS * b + PACK * m0 : PASS * b + PACK * m1])
 
-        def gather_words(u, g, pieces=1):
-            width = S // pieces
-            for i in range(pieces):
-                offsets = lists[u][:, width * i // 16 : width * (i + 1) // 16]
-                nc.vector.tensor_copy(picked[u][g][:, width * i : width * (i + 1)], table[g][:].bitcast(U32).indirect(offsets))
+        def load_later(b, g):
+            load_w(b, g, w_later, [PLACE[b, g, c] for c in range(len(LOADS[b, g]))])
 
-        def gather_scales(u):
-            nc.vector.tensor_copy(staged_scale[:, S * u : S * (u + 1)], table_scale[:].indirect(lists[u][:]))
+        def place_rows(target, q, g, c0, c1):
+            row = 16 * g + ROWS * q
+            nc.sync.dma_start(out=target.bitcast(I32), in_=picked_scale[row : row + ROWS, c0:c1].bitcast(I32))
 
-        def cast_w(b, g, c, parts=1):
-            m0, m1, ms = CHUNKS[b, g][c]
-            src = w_raw[b, g, c].rearrange("p j (m e t) -> p m j e t", e=2, t=PACK)
-            if b == 1:
-                dealt = w_bf[b, g, c][:].rearrange("p t (m e) j -> p m j e t", e=2)
-                m0, m1, ms = 0, m1 - m0, ms - m0
-            else:
-                dealt = w_bf[b, g][:].rearrange("p t (m e) j -> p m j e t", e=2)
-            h0, h1, hs = m0 // 2, m1 // 2, ms // 2
+        def place_planes(quadrants):
+            for q in quadrants:
+                place_rows(planes[32 * q : 32 * q + ROWS, 0 : S + V], q, 0, 0, S + V)
+                place_rows(planes[32 * q + ROWS : 32 * q + 2 * ROWS, 0:S], q, 1, 0, S)
+
+        def round_w(b, g, c, parts):
+            m0, m1, ms = LOADS[b, g][c]
+            raw = w_raw[b, g, c].rearrange("p j (m e t) -> p m j e t", e=2, t=PACK)
+            dealt = w_bf[b, g, c][:].rearrange("p t (m e) j -> p m j e t", e=2)
+            split, end = (ms - m0) // 2, (m1 - m0) // 2
             width = PACK // parts
             for i in range(parts):
                 outs = slice(width * i, width * (i + 1))
-                if hs > h0:
-                    nc.vector.tensor_copy(out=dealt[:, h0:hs, :, :, outs], in_=src[:, 0 : hs - h0, :, :, outs])
-                if h1 > hs:
-                    nc.scalar.copy(out=dealt[:, hs:h1, :, :, outs], in_=src[:, hs - h0 : h1 - h0, :, :, outs])
+                nc.vector.tensor_copy(out=dealt[:, 0:split, :, :, outs], in_=raw[:, 0:split, :, :, outs])
+                if split < end:
+                    nc.scalar.copy(out=dealt[:, split:end, :, :, outs], in_=raw[:, split:end, :, :, outs])
 
-        def quantize_w(b, g, pieces):
-            flat = w_bf[b, g][:].rearrange("p t m j -> p (t m j)")
-            width = PASS // pieces
-            for i in range(pieces):
+        def quantize_whole(g, parts):
+            flat = w_bf[0, g, 0][:].rearrange("p t m j -> p (t m j)")
+            width = PASS // parts
+            for i in range(parts):
                 cols = slice(width * i, width * (i + 1))
                 nc.vector.quantize_mx(
-                    out=w_q[b, g][:, cols].bitcast(FP8X4),
-                    scales=w_s[b, g][:, cols],
+                    out=w_q[0, g][:, cols].bitcast(FP8X4),
+                    scales=w_s[0, g][:, cols],
                     in_=flat[:, PACK * width * i : PACK * width * (i + 1)],
                 )
 
         def quantize_half(g, c):
-            half = P // 2
-            for t in range(PACK):
-                cols = slice(P * t + half * c, P * t + half * (c + 1))
+            for j in range(PACK):
+                cols = slice(P * j + HALF * c, P * j + HALF * (c + 1))
                 nc.vector.quantize_mx(
                     out=w_q[1, g][:, cols].bitcast(FP8X4),
                     scales=w_s[1, g][:, cols],
-                    in_=w_bf[1, g, c][:, t].rearrange("p m j -> p (m j)"),
+                    in_=w_bf[1, g, c][:, j].rearrange("p m j -> p (m j)"),
                 )
 
-        z_bank, z_bf, z_q, z_s = {}, {}, {}, {}
-
-        def z_pass(b, t, j, g, ends=((0, 0), (PACK - 1, PASSES - 1))):
+        def z_pass(b, t, j, g, first=(0, 0), last=(PACK - 1, PASSES - 1)):
             if (b, t) not in z_bank:
                 z_bank[b, t] = psum.tile([P, PACK, P], F32, name=f"z_bank{b}{t}", tag=f"bank{b}{t}")
             cols = slice(P * j, P * (j + 1))
@@ -151,146 +129,131 @@ def tile_picked_zresc_sig_p_kernel(tc, x_words, x_scales, w1, offs, dst, out):
                 lhsT=w_q[b, g][:, cols].bitcast(FP8X4),
                 lhsT_scale=w_s[b, g][:, cols],
                 rhs=picked[0][g][:, toks].bitcast(FP8X4),
-                rhs_scale=planes[4 * g : P, toks],
-                start=((j, g) == ends[0]),
-                stop=((j, g) == ends[1]),
+                rhs_scale=planes[ROWS * g : P, toks],
+                start=((j, g) == first),
+                stop=((j, g) == last),
             )
 
-        def z_round(b, t, engine_copy):
-            first, count = z_group(b, t)
-            if b == 0:
-                start = 2 * PASS * LATER[1, 0, 1]
-                z_bf[b, first] = later[0][:, start : start + 8 * P].bitcast(BF16).rearrange("p (n j) -> p n j", j=PACK)
-            elif t == first:
-                tag = "z_bf10" if (b, t) == (1, 3) else f"z_bf{b}{t}"
-                own = keep.tile([P, count * P, PACK], BF16, name=f"z_bf{b}{t}", tag=tag, align_bytes=256)
-                z_bf[b, first] = own[:]
-            toks = slice(P * (t - first), P * (t - first + 1))
-            engine_copy(out=z_bf[b, first][:, toks, :], in_=z_bank[b, t][:].rearrange("p j n -> p n j"))
+        def close_first_two(b):
+            for pair in (0, 2):
+                for t in (0, 1):
+                    z_pass(b, t, pair, 1)
+                    z_pass(b, t, pair + 1, 1)
 
-        def z_group(b, t):
-            return (0, TILES) if b == 0 else (t, 1)
+        def round_z(b, t, copy, target):
+            copy(out=target, in_=z_bank[b, t][:].rearrange("p j n -> p n j"))
 
-        def z_quantize(b, first):
-            count = z_group(b, first)[1]
-            if b == 0:
-                if first == 0:
-                    held.append(keep.tile([P, S], U32, name="z_q0", tag="w_bf111", align_bytes=256))
-                codes = held[0][:, P * first : P * (first + count)]
-            else:
-                own = keep.tile([P, P], U32, name=f"z_q{b}{first}", align_bytes=256)
-                codes = own[:]
-            scales = keep.tile([P, count * P], U8, name=f"z_s{b}{first}", align_bytes=256)
-            nc.vector.quantize_mx(
-                out=codes.bitcast(FP8X4),
-                scales=scales[:],
-                in_=z_bf[b, first].rearrange("p n j -> p (n j)"),
-            )
-            for i in range(count):
-                z_q[b, first + i] = codes[:, P * i : P * (i + 1)]
-                z_s[b, first + i] = scales[:, P * i : P * (i + 1)]
+        def round_second(t, copy, tag):
+            own = keep.tile([P, P, PACK], BF16, name=f"z_bf1{t}", tag=tag, align_bytes=ALIGN)
+            z_bf[t] = own[:]
+            round_z(1, t, copy, z_bf[t])
 
-        def y_pass(b, t, i=0):
-            tag, c0, c1 = PIECES[t][i]
-            if (t, i) not in y_bank:
-                y_bank[t, i] = psum.tile([P, c1 - c0], F32, name=f"y_bank{t}{i}", tag=tag)
-            nc.tensor.matmul_mx(
-                out=y_bank[t, i][:],
-                lhsT=z_q[b, t].bitcast(FP8X4),
-                lhsT_scale=z_s[b, t],
-                rhs=picked[1][b][:, c0:c1].bitcast(FP8X4),
-                rhs_scale=planes[:, S + c0 : S + c1] if b == 0 else last_plane[:, c0:c1],
-                start=(b == 0),
-                stop=(b == PASSES - 1),
-            )
+        def quantize_z(b, tiles, rounded, tag):
+            width = len(tiles) * P
+            codes = keep.tile([P, width], U32, name=f"z_q{b}{tiles[0]}", tag=tag, align_bytes=ALIGN)
+            scales = keep.tile([P, width], U8, name=f"z_s{b}{tiles[0]}", align_bytes=ALIGN)
+            nc.vector.quantize_mx(out=codes[:].bitcast(FP8X4), scales=scales[:], in_=rounded.rearrange("p n j -> p (n j)"))
+            for i, t in enumerate(tiles):
+                z_q[b, t] = codes[:, P * i : P * (i + 1)]
+                z_s[b, t] = scales[:, P * i : P * (i + 1)]
 
-        def finish(t, i, pieces):
-            tag, c0, c1 = PIECES[t][i]
-            width = (c1 - c0) // pieces
-            for h in range(pieces):
-                result = keep.tile([P, width], F32, name=f"result{t}{i}{h}", align_bytes=256)
-                nc.scalar.activation(out=result[:], in_=y_bank[t, i][:, width * h : width * (h + 1)], func=SIGMOID)
-                nc.sync.dma_start(out=out[P * t : P * (t + 1), c0 + width * h : c0 + width * (h + 1)], in_=result[:])
+        def quantize_second(t):
+            quantize_z(1, [t], z_bf[t], f"z_q1{t}")
 
-        warm = keep.tile([P, 16], F32, name="warm")
-        nc.gpsimd.memset(warm[:, 0:8], 0.0)
-        nc.scalar.activation(out=warm[:, 8:16], in_=warm[:, 0:8], func=SIGMOID)
+        def y_passes(t):
+            for b in range(PASSES):
+                for i, (tag, c0, c1) in enumerate(Y_BANKS[t]):
+                    if b == 0:
+                        y_bank[t, i] = psum.tile([P, c1 - c0], F32, name=f"y_bank{t}{i}", tag=tag)
+                    nc.tensor.matmul_mx(
+                        out=y_bank[t, i][:],
+                        lhsT=z_q[b, t].bitcast(FP8X4),
+                        lhsT_scale=z_s[b, t],
+                        rhs=picked[1][b][:, c0:c1].bitcast(FP8X4),
+                        rhs_scale=planes[:, S + c0 : S + c1] if b == 0 else last_plane[:, c0:c1],
+                        start=(b == 0),
+                        stop=(b == PASSES - 1),
+                    )
+
+        preload = keep.tile([P, 16], F32, name="preload")
+        nc.gpsimd.memset(preload[:, 0:8], 0.0)
+        nc.scalar.activation(out=preload[:, 8:16], in_=preload[:, 0:8], func=SIGMOID)
+
         nc.vector.memset(table_scale[32:64, :].bitcast(I32), 0)
         nc.vector.memset(table_scale[64:P, :].bitcast(I32), 0)
         nc.vector.memset(planes[:].bitcast(I32), 0)
         nc.vector.memset(last_plane[:].bitcast(I32), 0)
-        load_scales()
+
+        nc.sync.dma_start(out=table_scale[0:32, :].bitcast(I32), in_=x_scales.rearrange("g q n -> (g q) n").bitcast(I32))
         nc.sync.dma_start(lists[0][:], offs)
         nc.sync.dma_start(lists[1][:], dst)
-        load_table(0)
-        load_table(1)
-        load_w(0, 0)
-        gather_scales(0)
-        gather_scales(1)
-        place_scales((0, 2))
-        load_w(0, 1)
-        place_scales((1, 3))
-        gather_words(0, 0)
-        gather_words(1, 0)
-        gather_words(0, 1)
-        gather_words(1, 1)
-        load_w(1, 0)
+        for g in range(PASSES):
+            load_table(g)
+        w_first = wide.tile([P, PACK * PASS], F32, name="w_first", align_bytes=ROW_ALIGN)
+        load_w(0, 0, w_first, [0])
+        for u in range(2):
+            nc.vector.tensor_copy(picked_scale[:, S * u : S * (u + 1)], table_scale[:].indirect(lists[u][:]))
 
-        def closing(b, rest):
-            for half in (0, 2):
-                for t in (0, 1):
-                    z_pass(b, t, half, 1)
-                    z_pass(b, t, half + 1, 1)
-            for t in rest:
-                for j in range(PACK):
-                    z_pass(b, t, j, 1)
+        place_planes((0, 2))
+        w_later = wide.tile([P, 6 * HALF_PART], F32, name="w_later", tag="scale_rows", align_bytes=ROW_ALIGN)
+        load_later(0, 1)
+        place_planes((1, 3))
+        for g in range(PASSES):
+            for u in range(2):
+                nc.vector.tensor_copy(picked[u][g][:, 0:S], table[g][:].bitcast(U32).indirect(lists[u][:, 0 : S // 16]))
+        load_later(1, 0)
 
-        cast_w(0, 0, 0)
-        quantize_w(0, 0, 1)
-        for t in range(2):
+        round_w(0, 0, 0, 1)
+        quantize_whole(0, 1)
+        for t in (0, 1):
             for j in range(PACK):
                 z_pass(0, t, j, 0)
-        cast_w(0, 1, 0, 2)
-        load_w(1, 1)
+        round_w(0, 1, 0, 2)
+        load_later(1, 1)
         for q in (0, 2, 1, 3):
-            nc.sync.dma_start(out=last_plane[32 * q : 32 * q + 4, :].bitcast(I32), in_=staged_scale[16 + 4 * q : 20 + 4 * q, S : 2 * S].bitcast(I32))
-        quantize_w(0, 1, 2)
-        closing(0, ())
+            place_rows(last_plane[32 * q : 32 * q + ROWS, :], q, 1, S, S + V)
+        quantize_whole(1, 2)
+        close_first_two(0)
         for t in (2, 3):
             for g in reversed(range(PASSES)):
                 for j in reversed(range(PACK)):
-                    z_pass(0, t, j, g, ((PACK - 1, PASSES - 1), (0, 0)))
-        cast_w(1, 0, 0, 2)
+                    z_pass(0, t, j, g, first=(PACK - 1, PASSES - 1), last=(0, 0))
+
+        round_w(1, 0, 0, 2)
         quantize_half(0, 0)
-        cast_w(1, 0, 1, 2)
+        round_w(1, 0, 1, 2)
+        start = HALF_PART * PLACE[1, 0, 1]
+        z_first = w_later[:, start : start + HALF_PART].bitcast(BF16).rearrange("p (n j) -> p n j", j=PACK)
         for t in range(TILES):
-            z_round(0, t, nc.scalar.copy)
+            round_z(0, t, nc.scalar.copy, z_first[:, P * t : P * (t + 1), :])
         quantize_half(0, 1)
         for t in range(TILES):
             for j in range(PACK):
                 z_pass(1, t, j, 0)
-        cast_w(1, 1, 0, 2)
-        quantize_half(1, 0)
-        cast_w(1, 1, 1, 2)
-        quantize_half(1, 1)
-        closing(1, (2, 3))
-        z_quantize(0, 0)
-        z_round(1, 0, nc.scalar.copy)
-        z_round(1, 1, nc.vector.tensor_copy)
-        z_round(1, 2, nc.scalar.copy)
-        z_quantize(1, 0)
-        for b in range(PASSES):
-            for i in range(2):
-                y_pass(b, 0, i)
-        z_quantize(1, 1)
-        y_pass(0, 1)
-        y_pass(1, 1)
-        z_round(1, 3, nc.vector.tensor_copy)
+        for c in range(2):
+            round_w(1, 1, c, 2)
+            quantize_half(1, c)
+        close_first_two(1)
         for t in (2, 3):
-            z_quantize(1, t)
-            y_pass(0, t)
-            y_pass(1, t)
-        finish(0, 0, 1)
-        finish(0, 1, 1)
-        for t in range(1, TILES):
-            finish(t, 0, 2)
+            for j in range(PACK):
+                z_pass(1, t, j, 1)
+
+        quantize_z(0, list(range(TILES)), z_first, "w_bf111")
+        round_second(0, nc.scalar.copy, "z_bf10")
+        round_second(1, nc.vector.tensor_copy, "z_bf11")
+        round_second(2, nc.scalar.copy, "z_bf12")
+        for t in (0, 1):
+            quantize_second(t)
+            y_passes(t)
+        round_second(3, nc.vector.tensor_copy, "z_bf10")
+        for t in (2, 3):
+            quantize_second(t)
+            y_passes(t)
+
+        for t in range(TILES):
+            for h in range(2):
+                cols = slice(h * V // 2, (h + 1) * V // 2)
+                source = y_bank[t, h][:, 0 : V // 2] if len(Y_BANKS[t]) == 2 else y_bank[t, 0][:, cols]
+                result = wide.tile([P, V // 2], F32, name=f"result{t}{h}", align_bytes=ROW_ALIGN)
+                nc.scalar.activation(out=result[:], in_=source, func=SIGMOID)
+                nc.sync.dma_start(out=out[P * t : P * (t + 1), cols], in_=result[:])

from contextlib import ExitStack

import concourse.mybir as mybir

F32 = mybir.dt.float32
BF16 = mybir.dt.bfloat16
I32 = mybir.dt.int32
U32 = mybir.dt.uint32
U16 = mybir.dt.uint16
U8 = mybir.dt.uint8
FP8X4 = mybir.dt.float8_e4m3fn_x4
SIGMOID = mybir.ActivationFunctionType.Sigmoid

P = 128
PACK = 4
PASS = P * PACK
K, T, S, V = 1024, 2048, 512, 512
PASSES = K // PASS
TILES = S // P
HALF = P // 2
ROWS = 4
ALIGN = 256
ROW_ALIGN = 2048
FLOPS = 2 * K * K * S + 2 * K * S * V

LOADS = {
    (0, 0): [(0, 128, 56)],
    (0, 1): [(0, 128, 84)],
    (1, 0): [(0, 64, 32), (64, 128, 104)],
    (1, 1): [(0, 64, 64), (64, 128, 128)],
}
PLACE = {(0, 1, 0): 0, (1, 0, 0): 2, (1, 1, 0): 3, (1, 0, 1): 4, (1, 1, 1): 5}
HALF_PART = PACK * PASS // 2
Y_BANKS = {
    0: [("bank00", 0, V // 2), ("bank02", V // 2, V)],
    1: [("bank01", 0, V)],
    2: [("bank12", 0, V)],
    3: [("bank13", 0, V)],
}


def tile_picked_zresc_sig_p_kernel(tc, x_words, x_scales, w1, offs, dst, out):
    nc = tc.nc
    with ExitStack() as ctx:
        keep = ctx.enter_context(tc.tile_pool(name="keep", bufs=1))
        wide = ctx.enter_context(tc.tile_pool(name="wide", bufs=1))
        psum = ctx.enter_context(tc.psum_pool(name="psum", bufs=1))

        lists = [
            keep.tile([P, S // 16], U16, name="offs_sb", align_bytes=ALIGN),
            keep.tile([P, V // 16], U16, name="dst_sb", align_bytes=ALIGN),
        ]
        table_scale = wide.tile([P, T], U8, name="table_scale", tag="scale_rows", align_bytes=ROW_ALIGN)
        picked = [[keep.tile([P, S], U32, name=f"picked{u}{g}", align_bytes=ALIGN) for g in range(PASSES)] for u in range(2)]
        picked_scale = keep.tile([P, S + V], U8, name="picked_scale", align_bytes=ALIGN)
        planes = keep.tile([P, S + V], U8, name="planes", align_bytes=ALIGN)
        last_plane = keep.tile([P, V], U8, name="last_plane", align_bytes=ALIGN)
        w_bf, w_q, w_s = {}, {}, {}
        for (b, g), loads in LOADS.items():
            for c, (m0, m1, ms) in enumerate(loads):
                name = f"w_bf{b}{g}{c}"
                w_bf[b, g, c] = keep.tile([P, PACK, m1 - m0, PACK], BF16, name=name, tag=name, align_bytes=ALIGN)
            w_q[b, g] = keep.tile([P, PASS], U32, name=f"w_q{b}{g}", align_bytes=ALIGN)
            w_s[b, g] = keep.tile([P, PASS], U8, name=f"w_s{b}{g}", align_bytes=ALIGN)
        table, w_raw, z_bank, z_bf, z_q, z_s, y_bank = {}, {}, {}, {}, {}, {}, {}

        def load_table(g):
            table[g] = wide.tile([P, T], I32, name=f"table{g}", align_bytes=ROW_ALIGN)
            nc.sync.dma_start(out=table[g][:], in_=x_words[g].rearrange("p n r -> p (n r)").bitcast(I32))

        def load_w(b, g, tile, places):
            rows = w1[PASS * g : PASS * (g + 1), :].rearrange("(p j) c -> p j c", j=PACK)
            for c, (m0, m1, ms) in enumerate(LOADS[b, g]):
                start = HALF_PART * places[c]
                w_raw[b, g, c] = tile[:, start : start + PACK * PACK * (m1 - m0)].rearrange("p (j c) -> p j c", j=PACK)
                nc.sync.dma_start(out=w_raw[b, g, c], in_=rows[:, :, PASS * b + PACK * m0 : PASS * b + PACK * m1])

        def load_later(b, g):
            load_w(b, g, w_later, [PLACE[b, g, c] for c in range(len(LOADS[b, g]))])

        def place_rows(target, q, g, c0, c1):
            row = 16 * g + ROWS * q
            nc.sync.dma_start(out=target.bitcast(I32), in_=picked_scale[row : row + ROWS, c0:c1].bitcast(I32))

        def place_planes(quadrants):
            for q in quadrants:
                place_rows(planes[32 * q : 32 * q + ROWS, 0 : S + V], q, 0, 0, S + V)
                place_rows(planes[32 * q + ROWS : 32 * q + 2 * ROWS, 0:S], q, 1, 0, S)

        def round_w(b, g, c, parts):
            m0, m1, ms = LOADS[b, g][c]
            raw = w_raw[b, g, c].rearrange("p j (m e t) -> p m j e t", e=2, t=PACK)
            dealt = w_bf[b, g, c][:].rearrange("p t (m e) j -> p m j e t", e=2)
            split, end = (ms - m0) // 2, (m1 - m0) // 2
            width = PACK // parts
            for i in range(parts):
                outs = slice(width * i, width * (i + 1))
                nc.vector.tensor_copy(out=dealt[:, 0:split, :, :, outs], in_=raw[:, 0:split, :, :, outs])
                if split < end:
                    nc.scalar.copy(out=dealt[:, split:end, :, :, outs], in_=raw[:, split:end, :, :, outs])

        def quantize_whole(g, parts):
            flat = w_bf[0, g, 0][:].rearrange("p t m j -> p (t m j)")
            width = PASS // parts
            for i in range(parts):
                cols = slice(width * i, width * (i + 1))
                nc.vector.quantize_mx(
                    out=w_q[0, g][:, cols].bitcast(FP8X4),
                    scales=w_s[0, g][:, cols],
                    in_=flat[:, PACK * width * i : PACK * width * (i + 1)],
                )

        def quantize_half(g, c):
            for j in range(PACK):
                cols = slice(P * j + HALF * c, P * j + HALF * (c + 1))
                nc.vector.quantize_mx(
                    out=w_q[1, g][:, cols].bitcast(FP8X4),
                    scales=w_s[1, g][:, cols],
                    in_=w_bf[1, g, c][:, j].rearrange("p m j -> p (m j)"),
                )

        def z_pass(b, t, j, g, first=(0, 0), last=(PACK - 1, PASSES - 1)):
            if (b, t) not in z_bank:
                z_bank[b, t] = psum.tile([P, PACK, P], F32, name=f"z_bank{b}{t}", tag=f"bank{b}{t}")
            cols = slice(P * j, P * (j + 1))
            toks = slice(P * t, P * (t + 1))
            nc.tensor.matmul_mx(
                out=z_bank[b, t][:, j, :],
                lhsT=w_q[b, g][:, cols].bitcast(FP8X4),
                lhsT_scale=w_s[b, g][:, cols],
                rhs=picked[0][g][:, toks].bitcast(FP8X4),
                rhs_scale=planes[ROWS * g : P, toks],
                start=((j, g) == first),
                stop=((j, g) == last),
            )

        def close_first_two(b):
            for pair in (0, 2):
                for t in (0, 1):
                    z_pass(b, t, pair, 1)
                    z_pass(b, t, pair + 1, 1)

        def round_z(b, t, copy, target):
            copy(out=target, in_=z_bank[b, t][:].rearrange("p j n -> p n j"))

        def round_second(t, copy, tag):
            own = keep.tile([P, P, PACK], BF16, name=f"z_bf1{t}", tag=tag, align_bytes=ALIGN)
            z_bf[t] = own[:]
            round_z(1, t, copy, z_bf[t])

        def quantize_z(b, tiles, rounded, tag):
            width = len(tiles) * P
            codes = keep.tile([P, width], U32, name=f"z_q{b}{tiles[0]}", tag=tag, align_bytes=ALIGN)
            scales = keep.tile([P, width], U8, name=f"z_s{b}{tiles[0]}", align_bytes=ALIGN)
            nc.vector.quantize_mx(out=codes[:].bitcast(FP8X4), scales=scales[:], in_=rounded.rearrange("p n j -> p (n j)"))
            for i, t in enumerate(tiles):
                z_q[b, t] = codes[:, P * i : P * (i + 1)]
                z_s[b, t] = scales[:, P * i : P * (i + 1)]

        def quantize_second(t):
            quantize_z(1, [t], z_bf[t], f"z_q1{t}")

        def y_passes(t):
            for b in range(PASSES):
                for i, (tag, c0, c1) in enumerate(Y_BANKS[t]):
                    if b == 0:
                        y_bank[t, i] = psum.tile([P, c1 - c0], F32, name=f"y_bank{t}{i}", tag=tag)
                    nc.tensor.matmul_mx(
                        out=y_bank[t, i][:],
                        lhsT=z_q[b, t].bitcast(FP8X4),
                        lhsT_scale=z_s[b, t],
                        rhs=picked[1][b][:, c0:c1].bitcast(FP8X4),
                        rhs_scale=planes[:, S + c0 : S + c1] if b == 0 else last_plane[:, c0:c1],
                        start=(b == 0),
                        stop=(b == PASSES - 1),
                    )

        preload = keep.tile([P, 16], F32, name="preload")
        nc.gpsimd.memset(preload[:, 0:8], 0.0)
        nc.scalar.activation(out=preload[:, 8:16], in_=preload[:, 0:8], func=SIGMOID)

        nc.vector.memset(table_scale[32:64, :].bitcast(I32), 0)
        nc.vector.memset(table_scale[64:P, :].bitcast(I32), 0)
        nc.vector.memset(planes[:].bitcast(I32), 0)
        nc.vector.memset(last_plane[:].bitcast(I32), 0)

        nc.sync.dma_start(out=table_scale[0:32, :].bitcast(I32), in_=x_scales.rearrange("g q n -> (g q) n").bitcast(I32))
        nc.sync.dma_start(lists[0][:], offs)
        nc.sync.dma_start(lists[1][:], dst)
        for g in range(PASSES):
            load_table(g)
        w_first = wide.tile([P, PACK * PASS], F32, name="w_first", align_bytes=ROW_ALIGN)
        load_w(0, 0, w_first, [0])
        for u in range(2):
            nc.vector.tensor_copy(picked_scale[:, S * u : S * (u + 1)], table_scale[:].indirect(lists[u][:]))

        place_planes((0, 2))
        w_later = wide.tile([P, 6 * HALF_PART], F32, name="w_later", tag="scale_rows", align_bytes=ROW_ALIGN)
        load_later(0, 1)
        place_planes((1, 3))
        for g in range(PASSES):
            for u in range(2):
                nc.vector.tensor_copy(picked[u][g][:, 0:S], table[g][:].bitcast(U32).indirect(lists[u][:, 0 : S // 16]))
        load_later(1, 0)

        round_w(0, 0, 0, 1)
        quantize_whole(0, 1)
        for t in (0, 1):
            for j in range(PACK):
                z_pass(0, t, j, 0)
        round_w(0, 1, 0, 2)
        load_later(1, 1)
        for q in (0, 2, 1, 3):
            place_rows(last_plane[32 * q : 32 * q + ROWS, :], q, 1, S, S + V)
        quantize_whole(1, 2)
        close_first_two(0)
        for t in (2, 3):
            for g in reversed(range(PASSES)):
                for j in reversed(range(PACK)):
                    z_pass(0, t, j, g, first=(PACK - 1, PASSES - 1), last=(0, 0))

        round_w(1, 0, 0, 2)
        quantize_half(0, 0)
        round_w(1, 0, 1, 2)
        start = HALF_PART * PLACE[1, 0, 1]
        z_first = w_later[:, start : start + HALF_PART].bitcast(BF16).rearrange("p (n j) -> p n j", j=PACK)
        for t in range(TILES):
            round_z(0, t, nc.scalar.copy, z_first[:, P * t : P * (t + 1), :])
        quantize_half(0, 1)
        for t in range(TILES):
            for j in range(PACK):
                z_pass(1, t, j, 0)
        for c in range(2):
            round_w(1, 1, c, 2)
            quantize_half(1, c)
        close_first_two(1)
        for t in (2, 3):
            for j in range(PACK):
                z_pass(1, t, j, 1)

        quantize_z(0, list(range(TILES)), z_first, "w_bf111")
        round_second(0, nc.scalar.copy, "z_bf10")
        round_second(1, nc.vector.tensor_copy, "z_bf11")
        round_second(2, nc.scalar.copy, "z_bf12")
        for t in (0, 1):
            quantize_second(t)
            y_passes(t)
        round_second(3, nc.vector.tensor_copy, "z_bf10")
        for t in (2, 3):
            quantize_second(t)
            y_passes(t)

        for t in range(TILES):
            for h in range(2):
                cols = slice(h * V // 2, (h + 1) * V // 2)
                source = y_bank[t, h][:, 0 : V // 2] if len(Y_BANKS[t]) == 2 else y_bank[t, 0][:, cols]
                result = wide.tile([P, V // 2], F32, name=f"result{t}{h}", align_bytes=ROW_ALIGN)
                nc.scalar.activation(out=result[:], in_=source, func=SIGMOID)
                nc.sync.dma_start(out=out[P * t : P * (t + 1), cols], in_=result[:])
